import numpy as np
import ml_dtypes


def mxq(x, axis, fmt="e4m3"):
    dtype, down = {"e4m3": (ml_dtypes.float8_e4m3fn, 7), "e5m2": (ml_dtypes.float8_e5m2, 14)}[fmt]
    v = np.moveaxis(np.asarray(x, np.float32).astype(ml_dtypes.bfloat16).astype(np.float64), axis, -1)
    blocks = v.reshape(v.shape[:-1] + (-1, 32))
    amax = np.abs(blocks).max(-1, keepdims=True)
    byte = np.maximum(np.where(amax > 0, np.frexp(amax)[1] - 1 + 127, 0) - down, 1)
    scale = np.exp2(byte - 127.0)
    codes = (blocks / scale).astype(np.float32).astype(dtype).astype(np.float64)
    return np.moveaxis((codes * scale).reshape(v.shape), -1, axis)


WIDE = False


def mx_kscale(k):
    if not WIDE:
        return np.ones(k)
    levels = np.array([10, -10, 5, -5, 0])
    if k % 512:
        return np.exp2(np.random.permutation(np.resize(levels, k // 32))).repeat(32)
    a = np.empty((k // 512, 16))
    for p in range(k // 512):
        a[p, :8] = np.random.permutation(np.resize(levels, 8))
        for g in range(8):
            far = levels[np.abs(levels - a[p, g]) >= 10]
            a[p, g + 8] = far[np.random.randint(len(far))]
    return np.exp2(a.ravel()).repeat(32)


def f64(x):
    return np.asarray(x).astype(np.float64)


def striped(idx):
    return np.tile(idx.reshape(-1, 16).T, (8, 1)).astype(np.uint16)


def unstriped(offs):
    return offs[:16].T.reshape(-1).astype(np.int64)


def striped8(idx):
    return np.concatenate([x.reshape(-1, 16).T for x in idx]).astype(np.uint16)


def runs(offs, k):
    lists = np.stack([offs[16 * r : 16 * r + 16].T.reshape(-1) for r in range(8)]).astype(np.int64)
    return lists[np.arange(k) % 512 // 64]


def pack_weight(w):
    k, n = w.shape
    w = f64(np.asarray(w, np.float32).astype(ml_dtypes.bfloat16)).reshape(k // 32, 32, n)
    amax = np.abs(w).max(1)
    byte = np.clip(np.where(amax > 0, np.frexp(amax)[1] - 1 + 127 - 7, 1), 1, 254)
    scaled = (w * np.exp2(127.0 - byte)[:, None, :]).reshape(k, n).astype(np.float32)
    words = np.ascontiguousarray(scaled.reshape(k // 512, 128, 4, n).transpose(0, 1, 3, 2)).astype(ml_dtypes.float8_e4m3fn).view(np.uint8)
    return words, np.ascontiguousarray(byte.astype(np.uint8).reshape(k // 512, 16, n))


def unpack_weight(words, scales):
    g, p, n, _ = words.shape
    vals = np.ascontiguousarray(words).view(ml_dtypes.float8_e4m3fn).astype(np.float64) * np.repeat(np.exp2(scales.astype(np.float64) - 127.0), 8, axis=1)[..., None]
    return vals.transpose(0, 1, 3, 2).reshape(g * 512, n)


E2M1 = np.array([0.0, 0.5, 1.0, 1.5, 2.0, 3.0, 4.0, 6.0, -0.0, -0.5, -1.0, -1.5, -2.0, -3.0, -4.0, -6.0])


def pack_fp4(w):
    k, n = w.shape
    w = f64(np.asarray(w, np.float32).astype(ml_dtypes.bfloat16)).reshape(k // 32, 32, n)
    amax = np.abs(w).max(1)
    mant, ex = np.frexp(amax / 6.0)
    byte = np.clip(np.where(amax > 0, np.where(mant > 0.5, ex, ex - 1) + 127, 1), 1, 254)
    scaled = (w * np.exp2(127.0 - byte)[:, None, :]).reshape(k, n).astype(np.float32)
    c = np.ascontiguousarray(scaled.reshape(k // 512, 128, 4, n).transpose(0, 1, 3, 2)).astype(ml_dtypes.float4_e2m1fn).view(np.uint8) & 0xF
    words = (c[..., 0::2] | (c[..., 1::2] << 4)).reshape(k // 512, 128, 2 * n)
    return np.ascontiguousarray(words), np.ascontiguousarray(byte.astype(np.uint8).reshape(k // 512, 16, n))


def unpack_fp4(words, scales):
    g, _, n = scales.shape
    words = np.ascontiguousarray(words).reshape(g, 128, n, 2)
    nib = np.empty((g, 128, n, 4), np.uint8)
    nib[..., 0::2] = words & 0xF
    nib[..., 1::2] = words >> 4
    vals = E2M1[nib] * np.repeat(np.exp2(scales.astype(np.float64) - 127.0), 8, axis=1)[..., None]
    return vals.transpose(0, 1, 3, 2).reshape(g * 512, n)


def planes(y):
    n, m = y.shape
    v = y.astype(np.float32).astype(ml_dtypes.bfloat16).astype(np.float64).reshape(n // 32, 32, m)
    top = np.abs(v).max(1)
    byte = np.clip(np.where(top > 0, np.frexp(top)[1] - 1 + 127 - 7, 1), 1, 254)
    codes = (v * np.exp2(127.0 - byte)[:, None, :]).reshape(n, m).astype(np.float32).astype(ml_dtypes.float8_e4m3fn).view(np.uint8)
    words = codes.reshape(n // 512, 128, 4, m).transpose(0, 1, 3, 2)
    return np.ascontiguousarray(words), np.ascontiguousarray(byte.astype(np.uint8).reshape(n // 512, 16, m))


K, T, S, N, H, W = 512, 2048, 512, 512, 512, 256


def setup_inputs():
    n = np.random.standard_normal
    s = mx_kscale(K)[:, None]
    u = mx_kscale(H)
    packed_xT = pack_weight(n((K, T)) * s)
    packed_w3 = pack_fp4(n((H, N)) / np.sqrt(H) / u[:, None])
    perm = np.stack([np.random.permutation(S) for _ in range(8)])
    return {
        "x_words": packed_xT[0],
        "x_scales": packed_xT[1],
        "w1": (n((K, H)) / np.sqrt(K) / s * u).astype(np.float32),
        "w2": (n((H, H)) / np.sqrt(H) / u[:, None] * u).astype(np.float32),
        "w3_words": packed_w3[0],
        "w3_scales": packed_w3[1],
        "res": n((N, S)).astype(np.float32),
        "offs": striped(np.random.permutation(T)[:S]),
        "n1": striped8(perm[:, :W]),
        "n2": striped8(perm[:, W:]),
        "n3": striped8(np.stack([np.random.permutation(S) for _ in range(8)])),
        "n4": striped8(np.stack([np.random.permutation(S) for _ in range(8)])),
    }


def reference(x_words, x_scales, w1, w2, w3_words, w3_scales, res, offs, n1, n2, n3, n4):
    xq = unpack_weight(x_words, x_scales)[:, unstriped(offs)]
    y = mxq(f64(w1), 0, "e4m3").T @ xq
    pa = y[np.arange(H)[:, None], runs(n1, H)]
    pb = y[np.arange(H)[:, None], runs(n2, H)]
    ra = np.maximum(pa, pb)
    z = y.copy()
    z[np.arange(H)[:, None], runs(n1, H)] = ra
    h = mxq(f64(w2), 0, "e4m3").T @ mxq(z, 0, "e4m3")
    pa2 = h[np.arange(H)[:, None], runs(n3, H)]
    pb2 = h[np.arange(H)[:, None], runs(n4, H)]
    z2 = np.maximum(np.maximum(h, pa2), pb2) - (0.5 * (np.minimum(np.minimum(h, pa2), pb2)))
    out_0 = f64(res) + (unpack_fp4(w3_words, w3_scales).T @ mxq(z2, 0, "e4m3"))
    return (out_0,) + planes(out_0)

@@ -1,0 +1,205 @@
+from contextlib import ExitStack
+
+import concourse.mybir as mybir
+
+F32 = mybir.dt.float32
+BF16 = mybir.dt.bfloat16
+I32 = mybir.dt.int32
+U32 = mybir.dt.uint32
+U16 = mybir.dt.uint16
+U8 = mybir.dt.uint8
+FP8X4 = mybir.dt.float8_e4m3fn_x4
+FP4X4 = mybir.dt.float4_e2m1fn_x4
+ALU = mybir.AluOpType
+
+P = 128
+T = 2048
+S = 512
+W = 256
+HALF = 256
+CHUNKS = ((0, 256), (256, 128), (384, 128))
+
+FLOPS = 805306368
+
+
+def tile_picked_deepfillrange_none_po_kernel(
+    tc, x_words, x_scales, w1, w2, w3_words, w3_scales, res, offs, n1, n2, n3, n4, out_0, out_1, out_2
+):
+    nc = tc.nc
+    with ExitStack() as ctx:
+        keep = ctx.enter_context(tc.tile_pool(name="keep", bufs=1))
+        psum = ctx.enter_context(tc.psum_pool(name="psum", bufs=1))
+
+        def sb(name, shape, dtype):
+            return keep.tile(shape, dtype, name=name, align_bytes=64)
+
+        def bank(i, name):
+            return psum.tile([P, 512], F32, name=name, tag="bank%d" % i)
+
+        def load_list(name, src, cols):
+            t = keep.tile([P, cols], U16, name=name)
+            nc.sync.dma_start(t[:], src)
+            return t
+
+        def load_scale_rows(eng, dst, src):
+            for q in range(4):
+                eng.dma_start(dst[32 * q : 32 * q + 4, :].bitcast(I32), src[0, 4 * q : 4 * q + 4, :].bitcast(I32))
+
+        def interleave(copy, dst, src):
+            copy(dst.rearrange("p (c i) t -> p c t i", i=4), src.rearrange("p t (c i) -> p c t i", i=4))
+
+        xs = sb("xs", [P, T], U8)
+        nc.gpsimd.memset(xs[:].bitcast(I32), 0)
+        w3s_raw = sb("w3s_raw", [P, S], U8)
+        nc.gpsimd.memset(w3s_raw[:].bitcast(I32), 0)
+
+        offs_t = load_list("offs_t", offs, 32)
+        xw = sb("xw", [P, T], U32)
+        nc.sync.dma_start(xw[:].bitcast(I32), x_words[0].rearrange("p c r -> p (c r)").bitcast(I32))
+        load_scale_rows(nc.scalar, xs, x_scales)
+        w1v = w1.rearrange("(p j) c -> p j c", j=4)
+        w1_raw = []
+        for h in range(2):
+            r = sb("w1_raw%d" % h, [P, 4, HALF], F32)
+            nc.sync.dma_start(r[:], w1v[:, :, h * HALF : (h + 1) * HALF])
+            w1_raw.append(r)
+        n1_t = load_list("n1_t", n1, 16)
+        n2_t = load_list("n2_t", n2, 16)
+        w2_raw = sb("w2_raw", [P, 4, S], F32)
+        nc.sync.dma_start(w2_raw[:], w2.rearrange("(p j) c -> p j c", j=4))
+        n3_t = load_list("n3_t", n3, 32)
+        n4_t = load_list("n4_t", n4, 32)
+        w3w_raw = sb("w3w_raw", [P, 2 * S], U8)
+        nc.sync.dma_start(w3w_raw[:].bitcast(I32), w3_words[0].bitcast(I32))
+        load_scale_rows(nc.sync, w3s_raw, w3_scales)
+        res_t = sb("res_t", [P, 4, S], F32)
+        nc.sync.dma_start(res_t[:], res.rearrange("(p t) c -> p t c", t=4))
+
+        xgs = sb("xgs", [P, S], U8)
+        nc.vector.tensor_copy(xgs[:], xs[:].indirect(offs_t[:]))
+        xg = sb("xg", [P, S], U32)
+        nc.vector.tensor_copy(xg[:], xw[:].indirect(offs_t[:]))
+
+        w1b = sb("w1b", [P, 4, P, 4], BF16)
+        for h, copy in enumerate((nc.scalar.copy, nc.vector.tensor_copy)):
+            copy(
+                w1b[:, :, 64 * h : 64 * h + 64, :].rearrange("p t m j -> p m t j"),
+                w1_raw[h][:].rearrange("p j (m t) -> p m t j", t=4),
+            )
+        w1q = sb("w1q", [P, S], U32)
+        w1s = sb("w1s", [P, S], U8)
+        w1f = w1b[:].rearrange("p t m j -> p (t m j)")
+        for a, b in ((0, 128), (128, 256), (256, 512)):
+            nc.vector.quantize_mx(out=w1q[:, a:b].bitcast(FP8X4), scales=w1s[:, a:b], in_=w1f[:, 4 * a : 4 * b])
+
+        zc = sb("zc", [P, 4, S], BF16)
+        for t in range(4):
+            acc = bank(t, "y_acc%d" % t)
+            cols = slice(t * P, (t + 1) * P)
+            nc.tensor.matmul_mx(
+                out=acc[:], lhsT=w1q[:, cols].bitcast(FP8X4), lhsT_scale=w1s[:, cols],
+                rhs=xg[:].bitcast(FP8X4), rhs_scale=xgs[:], start=True, stop=True,
+            )
+            y = sb("y%d" % t, [P, S], F32)
+            nc.scalar.copy(y[:], acc[:])
+            pa = sb("pa%d" % t, [P, W], F32)
+            pb = sb("pb%d" % t, [P, W], F32)
+            ra = sb("ra%d" % t, [P, W], F32)
+            nc.vector.tensor_copy(pa[:], y[:].indirect(n1_t[:]))
+            nc.vector.tensor_copy(pb[:], y[:].indirect(n2_t[:]))
+            nc.vector.tensor_tensor(ra[:], pa[:], pb[:], ALU.max)
+            nc.vector.tensor_copy(y[:].indirect(n1_t[:]), ra[:])
+            nc.scalar.copy(zc[:, t, :], y[:])
+
+        w2b = sb("w2b", [P, 4, P, 4], BF16)
+        nc.scalar.copy(w2b[:].rearrange("p t m j -> p m t j"), w2_raw[:].rearrange("p j (m t) -> p m t j", t=4))
+        w2q = sb("w2q", [P, S], U32)
+        w2s = sb("w2s", [P, S], U8)
+        nc.vector.quantize_mx(out=w2q[:].bitcast(FP8X4), scales=w2s[:], in_=w2b[:].rearrange("p t m j -> p (t m j)"))
+
+        w3w = sb("w3w", [P, 2 * S], U8)
+        nc.vector.tensor_copy(
+            w3w[:].rearrange("p (t m e) -> p m t e", t=4, e=2), w3w_raw[:].rearrange("p (m t e) -> p m t e", t=4, e=2)
+        )
+        w3s = sb("w3s", [P, S], U8)
+        nc.vector.tensor_copy(w3s[:].rearrange("p (t m) -> p m t", t=4), w3s_raw[:].rearrange("p (m t) -> p m t", t=4))
+
+        zb = [sb("zb%d" % h, [P, HALF, 4], BF16) for h in range(2)]
+        interleave(nc.vector.tensor_copy, zb[0][:], zc[:, :, 0:256])
+        interleave(nc.scalar.copy, zb[1][:, 0:128, :], zc[:, :, 256:384])
+        interleave(nc.vector.tensor_copy, zb[1][:, 128:256, :], zc[:, :, 384:512])
+        hw = [sb("hw%d" % t, [P, S], F32) for t in range(4)]
+        ha = [sb("ha%d" % c, [P, 4, n], F32) for c, (c0, n) in enumerate(CHUNKS)]
+        h_acc = {}
+        for h in range(2):
+            zq = sb("zq%d" % h, [P, HALF], U32)
+            zs = sb("zs%d" % h, [P, HALF], U8)
+            nc.vector.quantize_mx(out=zq[:].bitcast(FP8X4), scales=zs[:], in_=zb[h][:].rearrange("p c t -> p (c t)"))
+            for t in range(4):
+                acc = bank(4 * (1 - h) + t, "h_acc%d_%d" % (h, t))
+                cols = slice(t * P, (t + 1) * P)
+                nc.tensor.matmul_mx(
+                    out=acc[:, 0:HALF], lhsT=w2q[:, cols].bitcast(FP8X4), lhsT_scale=w2s[:, cols],
+                    rhs=zq[:].bitcast(FP8X4), rhs_scale=zs[:], start=True, stop=True,
+                )
+                h_acc[(h, t)] = acc
+        for t in range(4):
+            for h in range(2):
+                nc.scalar.copy(hw[t][:, h * HALF : (h + 1) * HALF], h_acc[(h, t)][:, 0:HALF])
+        for c, (c0, n) in enumerate(CHUNKS):
+            for t in range(4):
+                lo = c0 % HALF
+                nc.scalar.copy(ha[c][:, t, :], h_acc[(c0 // HALF, t)][:, lo : lo + n])
+
+        oq = sb("oq", [P, S], U32)
+        osc = sb("osc", [P, S], U8)
+        out0v = out_0.rearrange("(p t) c -> p t c", t=4)
+        out1v = out_1[0].rearrange("p c r -> p (c r)").bitcast(I32)
+        for c, (c0, n) in enumerate(CHUNKS):
+            lists = slice(c0 // 16, (c0 + n) // 16)
+            cols = slice(c0, c0 + n)
+            gb = sb("gb%d" % c, [P, 4, n], F32)
+            gc = sb("gc%d" % c, [P, 4, n], F32)
+            for t in range(4):
+                nc.vector.tensor_copy(gb[:, t, :], hw[t][:].indirect(n3_t[:, lists]))
+                nc.vector.tensor_copy(gc[:, t, :], hw[t][:].indirect(n4_t[:, lists]))
+            hi1 = sb("hi1_%d" % c, [P, 4, n], F32)
+            lo1 = sb("lo1_%d" % c, [P, 4, n], F32)
+            hi2 = sb("hi2_%d" % c, [P, 4, n], F32)
+            lo2 = sb("lo2_%d" % c, [P, 4, n], F32)
+            nc.vector.tensor_tensor(hi1[:], ha[c][:], gb[:], ALU.max)
+            nc.vector.tensor_tensor(lo1[:], ha[c][:], gb[:], ALU.min)
+            nc.vector.tensor_tensor(hi2[:], hi1[:], gc[:], ALU.max)
+            nc.vector.tensor_tensor(lo2[:], lo1[:], gc[:], ALU.min)
+            z2c = sb("z2c%d" % c, [P, 4, n], BF16)
+            nc.vector.scalar_tensor_tensor(z2c[:], lo2[:], -0.5, hi2[:], ALU.mult, ALU.add)
+            z2b = sb("z2b%d" % c, [P, n, 4], BF16)
+            interleave(nc.scalar.copy, z2b[:], z2c[:])
+            z2q = sb("z2q%d" % c, [P, n], U32)
+            z2s = sb("z2s%d" % c, [P, n], U8)
+            nc.vector.quantize_mx(out=z2q[:].bitcast(FP8X4), scales=z2s[:], in_=z2b[:].rearrange("p c t -> p (c t)"))
+            o = sb("o%d" % c, [P, 4, n], F32)
+            per_bank = 512 // n
+            for g in range(4 // per_bank):
+                acc = bank(2 * c + g, "o_acc%d_%d" % (c, g))
+                for k in range(per_bank):
+                    t = g * per_bank + k
+                    nc.tensor.matmul_mx(
+                        out=acc[:, k * n : (k + 1) * n],
+                        lhsT=w3w[:, 256 * t : 256 * (t + 1)].bitcast(FP4X4), lhsT_scale=w3s[:, t * P : (t + 1) * P],
+                        rhs=z2q[:].bitcast(FP8X4), rhs_scale=z2s[:], start=True, stop=True,
+                    )
+                ts = slice(g * per_bank, (g + 1) * per_bank)
+                nc.vector.tensor_tensor(
+                    o[:, ts, :], acc[:].rearrange("p (k n) -> p k n", n=n), res_t[:, ts, cols], ALU.add
+                )
+            nc.sync.dma_start(out0v[:, :, cols], o[:])
+            ob = sb("ob%d" % c, [P, n, 4], BF16)
+            interleave(nc.scalar.copy, ob[:], o[:])
+            nc.vector.quantize_mx(
+                out=oq[:, cols].bitcast(FP8X4), scales=osc[:, cols], in_=ob[:].rearrange("p c t -> p (c t)")
+            )
+            nc.sync.dma_start(out1v[:, cols], oq[:, cols].bitcast(I32))
+        for q in range(4):
+            eng = nc.scalar if q % 2 else nc.sync
+            eng.dma_start(out_2[0, 4 * q : 4 * q + 4, :].bitcast(I32), osc[32 * q : 32 * q + 4, :].bitcast(I32))

@@ -1,6 +1,7 @@
 from contextlib import ExitStack
 
 import concourse.mybir as mybir
+from concourse.masks import make_identity
 
 F32 = mybir.dt.float32
 BF16 = mybir.dt.bfloat16
@@ -11,13 +12,15 @@ U8 = mybir.dt.uint8
 FP8X4 = mybir.dt.float8_e4m3fn_x4
 FP4X4 = mybir.dt.float4_e2m1fn_x4
 ALU = mybir.AluOpType
+ACT = mybir.ActivationFunctionType
 
 P = 128
 T = 2048
 S = 512
 W = 256
 HALF = 256
-CHUNKS = ((0, 256), (256, 128), (384, 128))
+NC = 128
+W1_SPLIT = 40
 
 FLOPS = 805306368
 
@@ -30,8 +33,8 @@ def tile_picked_deepfillrange_none_po_kernel(
         keep = ctx.enter_context(tc.tile_pool(name="keep", bufs=1))
         psum = ctx.enter_context(tc.psum_pool(name="psum", bufs=1))
 
-        def sb(name, shape, dtype):
-            return keep.tile(shape, dtype, name=name, align_bytes=64)
+        def sb(name, shape, dtype, tag=None):
+            return keep.tile(shape, dtype, name=name, tag=tag or name, align_bytes=64)
 
         def bank(i, name):
             return psum.tile([P, 512], F32, name=name, tag="bank%d" % i)
@@ -49,9 +52,12 @@ def tile_picked_deepfillrange_none_po_kernel(
             copy(dst.rearrange("p (c i) t -> p c t i", i=4), src.rearrange("p t (c i) -> p c t i", i=4))
 
         xs = sb("xs", [P, T], U8)
-        nc.gpsimd.memset(xs[:].bitcast(I32), 0)
+        nc.vector.memset(xs[:].bitcast(I32), 0)
         w3s_raw = sb("w3s_raw", [P, S], U8)
         nc.gpsimd.memset(w3s_raw[:].bitcast(I32), 0)
+
+        ident = sb("ident", [P, P], F32)
+        make_identity(nc, ident[:])
 
         offs_t = load_list("offs_t", offs, 32)
         xw = sb("xw", [P, T], U32)
@@ -81,10 +87,14 @@ def tile_picked_deepfillrange_none_po_kernel(
         nc.vector.tensor_copy(xg[:], xw[:].indirect(offs_t[:]))
 
         w1b = sb("w1b", [P, 4, P, 4], BF16)
-        for h, copy in enumerate((nc.scalar.copy, nc.vector.tensor_copy)):
+        for h, m0, m1, copy in (
+            (0, 0, 64, nc.scalar.copy),
+            (1, 0, W1_SPLIT, nc.vector.tensor_copy),
+            (1, W1_SPLIT, 64, nc.scalar.copy),
+        ):
             copy(
-                w1b[:, :, 64 * h : 64 * h + 64, :].rearrange("p t m j -> p m t j"),
-                w1_raw[h][:].rearrange("p j (m t) -> p m t j", t=4),
+                w1b[:, :, 64 * h + m0 : 64 * h + m1, :].rearrange("p t m j -> p m t j"),
+                w1_raw[h][:, :, 4 * m0 : 4 * m1].rearrange("p j (m t) -> p m t j", t=4),
             )
         w1q = sb("w1q", [P, S], U32)
         w1s = sb("w1s", [P, S], U8)
@@ -94,105 +104,134 @@ def tile_picked_deepfillrange_none_po_kernel(
 
         zc = sb("zc", [P, 4, S], BF16)
         for t in range(4):
-            acc = bank(t, "y_acc%d" % t)
             cols = slice(t * P, (t + 1) * P)
-            nc.tensor.matmul_mx(
-                out=acc[:], lhsT=w1q[:, cols].bitcast(FP8X4), lhsT_scale=w1s[:, cols],
-                rhs=xg[:].bitcast(FP8X4), rhs_scale=xgs[:], start=True, stop=True,
-            )
             y = sb("y%d" % t, [P, S], F32)
-            nc.scalar.copy(y[:], acc[:])
+            if t == 0:
+                parts = ((0, 0, HALF, nc.scalar.copy), (4, HALF, S, nc.vector.tensor_copy))
+            else:
+                parts = ((t, 0, S, nc.scalar.copy),)
+            for b, c0, c1, copy in parts:
+                acc = bank(b, "y_acc%d_%d" % (t, c0))
+                nc.tensor.matmul_mx(
+                    out=acc[:, 0 : c1 - c0], lhsT=w1q[:, cols].bitcast(FP8X4), lhsT_scale=w1s[:, cols],
+                    rhs=xg[:, c0:c1].bitcast(FP8X4), rhs_scale=xgs[:, c0:c1], start=True, stop=True,
+                )
+                copy(y[:, c0:c1], acc[:, 0 : c1 - c0])
             pa = sb("pa%d" % t, [P, W], F32)
-            pb = sb("pb%d" % t, [P, W], F32)
-            ra = sb("ra%d" % t, [P, W], F32)
-            nc.vector.tensor_copy(pa[:], y[:].indirect(n1_t[:]))
-            nc.vector.tensor_copy(pb[:], y[:].indirect(n2_t[:]))
-            nc.vector.tensor_tensor(ra[:], pa[:], pb[:], ALU.max)
-            nc.vector.tensor_copy(y[:].indirect(n1_t[:]), ra[:])
-            nc.scalar.copy(zc[:, t, :], y[:])
+            d = sb("d%d" % t, [P, W], F32)
+            r = sb("r%d" % t, [P, W], F32)
+            for k in range(2):
+                nc.vector.tensor_copy(pa[:, k * NC : (k + 1) * NC], y[:].indirect(n1_t[:, 8 * k : 8 * k + 8]))
+            for k in range(2):
+                part = slice(k * NC, (k + 1) * NC)
+                nc.vector.tensor_tensor(d[:, part], y[:].indirect(n2_t[:, 8 * k : 8 * k + 8]), pa[:, part], ALU.subtract)
+            nc.scalar.activation(r[:], d[:], ACT.Relu)
+            nc.vector.tensor_tensor(y[:].indirect(n1_t[:]), pa[:], r[:], ALU.add)
+            for h in range(2):
+                nc.scalar.copy(zc[:, t, h * HALF : (h + 1) * HALF], y[:, h * HALF : (h + 1) * HALF])
 
         w2b = sb("w2b", [P, 4, P, 4], BF16)
-        nc.scalar.copy(w2b[:].rearrange("p t m j -> p m t j"), w2_raw[:].rearrange("p j (m t) -> p m t j", t=4))
-        w2q = sb("w2q", [P, S], U32)
+        for k in range(4):
+            nc.scalar.copy(
+                w2b[:, :, 32 * k : 32 * k + 32, :].rearrange("p t m j -> p m t j"),
+                w2_raw[:, :, 128 * k : 128 * k + 128].rearrange("p j (m t) -> p m t j", t=4),
+            )
+        w2q = sb("w2q", [P, S], U32, tag="pa3")
         w2s = sb("w2s", [P, S], U8)
         nc.vector.quantize_mx(out=w2q[:].bitcast(FP8X4), scales=w2s[:], in_=w2b[:].rearrange("p t m j -> p (t m j)"))
-
-        w3w = sb("w3w", [P, 2 * S], U8)
-        nc.vector.tensor_copy(
-            w3w[:].rearrange("p (t m e) -> p m t e", t=4, e=2), w3w_raw[:].rearrange("p (m t e) -> p m t e", t=4, e=2)
-        )
-        w3s = sb("w3s", [P, S], U8)
-        nc.vector.tensor_copy(w3s[:].rearrange("p (t m) -> p m t", t=4), w3s_raw[:].rearrange("p (m t) -> p m t", t=4))
 
         zb = [sb("zb%d" % h, [P, HALF, 4], BF16) for h in range(2)]
         interleave(nc.vector.tensor_copy, zb[0][:], zc[:, :, 0:256])
         interleave(nc.scalar.copy, zb[1][:, 0:128, :], zc[:, :, 256:384])
         interleave(nc.vector.tensor_copy, zb[1][:, 128:256, :], zc[:, :, 384:512])
         hw = [sb("hw%d" % t, [P, S], F32) for t in range(4)]
-        ha = [sb("ha%d" % c, [P, 4, n], F32) for c, (c0, n) in enumerate(CHUNKS)]
-        h_acc = {}
+        ha = sb("ha", [P, 4, S], F32)
+        zq = [sb("zq%d" % h, [P, HALF], U32) for h in range(2)]
+        zs = [sb("zs%d" % h, [P, HALF], U8) for h in range(2)]
         for h in range(2):
-            zq = sb("zq%d" % h, [P, HALF], U32)
-            zs = sb("zs%d" % h, [P, HALF], U8)
-            nc.vector.quantize_mx(out=zq[:].bitcast(FP8X4), scales=zs[:], in_=zb[h][:].rearrange("p c t -> p (c t)"))
-            for t in range(4):
-                acc = bank(4 * (1 - h) + t, "h_acc%d_%d" % (h, t))
-                cols = slice(t * P, (t + 1) * P)
+            nc.vector.quantize_mx(
+                out=zq[h][:].bitcast(FP8X4), scales=zs[h][:], in_=zb[h][:].rearrange("p c t -> p (c t)")
+            )
+        for t in range(4):
+            cols = slice(t * P, (t + 1) * P)
+            for h in range(2):
+                acc = bank(4 * h + t, "h_acc%d_%d" % (h, t))
                 nc.tensor.matmul_mx(
                     out=acc[:, 0:HALF], lhsT=w2q[:, cols].bitcast(FP8X4), lhsT_scale=w2s[:, cols],
-                    rhs=zq[:].bitcast(FP8X4), rhs_scale=zs[:], start=True, stop=True,
+                    rhs=zq[h][:].bitcast(FP8X4), rhs_scale=zs[h][:], start=True, stop=True,
                 )
-                h_acc[(h, t)] = acc
-        for t in range(4):
-            for h in range(2):
-                nc.scalar.copy(hw[t][:, h * HALF : (h + 1) * HALF], h_acc[(h, t)][:, 0:HALF])
-        for c, (c0, n) in enumerate(CHUNKS):
-            for t in range(4):
-                lo = c0 % HALF
-                nc.scalar.copy(ha[c][:, t, :], h_acc[(c0 // HALF, t)][:, lo : lo + n])
+                nc.scalar.copy(hw[t][:, h * HALF : (h + 1) * HALF], acc[:, 0:HALF])
+            nc.scalar.copy(ha[:, t, 0:NC], hw[t][:, 0:NC])
+
+        w3w = sb("w3w", [P, 2 * S], U8, tag="zb1")
+        nc.vector.tensor_copy(
+            w3w[:].rearrange("p (t m e) -> p m t e", t=4, e=2), w3w_raw[:].rearrange("p (m t e) -> p m t e", t=4, e=2)
+        )
+        w3s = sb("w3s", [P, S], U8, tag="zb0")
+        nc.vector.tensor_copy(w3s[:].rearrange("p (t m) -> p m t", t=4), w3s_raw[:].rearrange("p (m t) -> p m t", t=4))
 
         oq = sb("oq", [P, S], U32)
         osc = sb("osc", [P, S], U8)
         out0v = out_0.rearrange("(p t) c -> p t c", t=4)
         out1v = out_1[0].rearrange("p c r -> p (c r)").bitcast(I32)
-        for c, (c0, n) in enumerate(CHUNKS):
-            lists = slice(c0 // 16, (c0 + n) // 16)
-            cols = slice(c0, c0 + n)
-            gb = sb("gb%d" % c, [P, 4, n], F32)
-            gc = sb("gc%d" % c, [P, 4, n], F32)
+        n = NC
+        for c in range(4):
+            lists = slice(8 * c, 8 * c + 8)
+            cols = slice(c * n, (c + 1) * n)
+            d1 = sb("d1_%d" % c, [P, 4, n], F32)
+            d2 = sb("d2_%d" % c, [P, 4, n], F32)
+            neg = sb("neg%d" % c, [P, 4, n], F32)
+            up = sb("up%d" % c, [P, 4, n], F32)
+            down = sb("down%d" % c, [P, 4, n], F32)
+            half = sb("half%d" % c, [P, 4, n], F32)
             for t in range(4):
-                nc.vector.tensor_copy(gb[:, t, :], hw[t][:].indirect(n3_t[:, lists]))
-                nc.vector.tensor_copy(gc[:, t, :], hw[t][:].indirect(n4_t[:, lists]))
-            hi1 = sb("hi1_%d" % c, [P, 4, n], F32)
-            lo1 = sb("lo1_%d" % c, [P, 4, n], F32)
-            hi2 = sb("hi2_%d" % c, [P, 4, n], F32)
-            lo2 = sb("lo2_%d" % c, [P, 4, n], F32)
-            nc.vector.tensor_tensor(hi1[:], ha[c][:], gb[:], ALU.max)
-            nc.vector.tensor_tensor(lo1[:], ha[c][:], gb[:], ALU.min)
-            nc.vector.tensor_tensor(hi2[:], hi1[:], gc[:], ALU.max)
-            nc.vector.tensor_tensor(lo2[:], lo1[:], gc[:], ALU.min)
-            z2c = sb("z2c%d" % c, [P, 4, n], BF16)
-            nc.vector.scalar_tensor_tensor(z2c[:], lo2[:], -0.5, hi2[:], ALU.mult, ALU.add)
-            z2b = sb("z2b%d" % c, [P, n, 4], BF16)
-            interleave(nc.scalar.copy, z2b[:], z2c[:])
+                nc.vector.tensor_tensor(d1[:, t, :], hw[t][:].indirect(n3_t[:, lists]), ha[:, t, cols], ALU.subtract)
+                nc.vector.tensor_tensor(d2[:, t, :], hw[t][:].indirect(n4_t[:, lists]), ha[:, t, cols], ALU.subtract)
+                if t % 2:
+                    ts = slice(t - 1, t + 1)
+                    nc.scalar.activation(neg[:, ts, :], d1[:, ts, :], ACT.Relu, scale=-0.5)
+            if c == 0:
+                for t in range(4):
+                    nc.scalar.copy(ha[:, t, NC:S], hw[t][:, NC:S])
+            nc.scalar.activation(half[:], ha[:, :, cols], ACT.Copy, scale=0.5)
+            sum_t = bank(3 * (c % 2), "sum_t%d" % c)
+            for t in range(4):
+                nc.tensor.matmul(
+                    sum_t[:, t * P : (t + 1) * P], half[:, t, :], ident[:], is_transpose=True, start=(t == 0), stop=False
+                )
+            for g in range(2):
+                ts = slice(2 * g, 2 * g + 2)
+                nc.vector.scalar_tensor_tensor(up[:, ts, :], d1[:, ts, :], 0.0, d2[:, ts, :], ALU.max, ALU.max)
+                nc.vector.scalar_tensor_tensor(down[:, ts, :], d2[:, ts, :], -0.5, neg[:, ts, :], ALU.mult, ALU.max)
+                for term in (up, down):
+                    for t in (2 * g, 2 * g + 1):
+                        nc.tensor.matmul(
+                            sum_t[:, t * P : (t + 1) * P], term[:, t, :], ident[:], is_transpose=True,
+                            start=False, stop=(term is down and t == 3),
+                        )
+            pairs = sb("pairs%d" % c, [P, 2, P, 2], BF16)
+            nc.scalar.copy(pairs[:], sum_t[:].rearrange("j (u e p) -> j u p e", u=2, e=2))
+            back = bank(3 * (c % 2) + 1, "back%d" % c)
+            words = pairs[:].rearrange("j u p e -> j (u p e)").bitcast(F32)
+            for u in range(2):
+                nc.tensor.transpose(back[:, u * P : (u + 1) * P], words[:, u * P : (u + 1) * P], ident[:])
+            z2b = sb("z2b%d" % c, [P, 4 * n], BF16)
+            nc.scalar.copy(
+                z2b[:].bitcast(F32).rearrange("p (j u) -> p j u", u=2),
+                back[:, 0 : 2 * P].rearrange("p (u j) -> p j u", u=2),
+            )
             z2q = sb("z2q%d" % c, [P, n], U32)
             z2s = sb("z2s%d" % c, [P, n], U8)
-            nc.vector.quantize_mx(out=z2q[:].bitcast(FP8X4), scales=z2s[:], in_=z2b[:].rearrange("p c t -> p (c t)"))
+            nc.vector.quantize_mx(out=z2q[:].bitcast(FP8X4), scales=z2s[:], in_=z2b[:])
             o = sb("o%d" % c, [P, 4, n], F32)
-            per_bank = 512 // n
-            for g in range(4 // per_bank):
-                acc = bank(2 * c + g, "o_acc%d_%d" % (c, g))
-                for k in range(per_bank):
-                    t = g * per_bank + k
-                    nc.tensor.matmul_mx(
-                        out=acc[:, k * n : (k + 1) * n],
-                        lhsT=w3w[:, 256 * t : 256 * (t + 1)].bitcast(FP4X4), lhsT_scale=w3s[:, t * P : (t + 1) * P],
-                        rhs=z2q[:].bitcast(FP8X4), rhs_scale=z2s[:], start=True, stop=True,
-                    )
-                ts = slice(g * per_bank, (g + 1) * per_bank)
-                nc.vector.tensor_tensor(
-                    o[:, ts, :], acc[:].rearrange("p (k n) -> p k n", n=n), res_t[:, ts, cols], ALU.add
+            acc = bank(3 * (c % 2) + 2, "o_acc%d" % c)
+            for t in range(4):
+                nc.tensor.matmul_mx(
+                    out=acc[:, t * n : (t + 1) * n],
+                    lhsT=w3w[:, 256 * t : 256 * (t + 1)].bitcast(FP4X4), lhsT_scale=w3s[:, t * P : (t + 1) * P],
+                    rhs=z2q[:].bitcast(FP8X4), rhs_scale=z2s[:], start=True, stop=True,
                 )
+            nc.vector.tensor_tensor(o[:], acc[:].rearrange("p (k n) -> p k n", n=n), res_t[:, :, cols], ALU.add)
             nc.sync.dma_start(out0v[:, :, cols], o[:])
             ob = sb("ob%d" % c, [P, n, 4], BF16)
             interleave(nc.scalar.copy, ob[:], o[:])

@@ -20,6 +20,7 @@ S = 512
 W = 256
 HALF = 256
 NC = 128
+STRETCHES = ((0, 128), (128, 128), (256, 128), (384, 128))
 W1_SPLIT = 40
 
 FLOPS = 805306368
@@ -53,38 +54,29 @@ def tile_picked_deepfillrange_none_po_kernel(
 
         xs = sb("xs", [P, T], U8)
         nc.vector.memset(xs[:].bitcast(I32), 0)
-        w3s_raw = sb("w3s_raw", [P, S], U8)
-        nc.gpsimd.memset(w3s_raw[:].bitcast(I32), 0)
-
         ident = sb("ident", [P, P], F32)
         make_identity(nc, ident[:])
+
+        w3s_raw = sb("w3s_raw", [P, S], U8)
+        nc.gpsimd.memset(w3s_raw[:].bitcast(I32), 0)
 
         offs_t = load_list("offs_t", offs, 32)
         xw = sb("xw", [P, T], U32)
         nc.sync.dma_start(xw[:].bitcast(I32), x_words[0].rearrange("p c r -> p (c r)").bitcast(I32))
-        load_scale_rows(nc.scalar, xs, x_scales)
-        w1v = w1.rearrange("(p j) c -> p j c", j=4)
-        w1_raw = []
-        for h in range(2):
-            r = sb("w1_raw%d" % h, [P, 4, HALF], F32)
-            nc.sync.dma_start(r[:], w1v[:, :, h * HALF : (h + 1) * HALF])
-            w1_raw.append(r)
         n1_t = load_list("n1_t", n1, 16)
+        load_scale_rows(nc.sync, xs, x_scales)
+        w1v = w1.rearrange("(p j) c -> p j c", j=4)
+        w1_raw = sb("w1_raw", [P, 2, 4, HALF], F32)
+        for h in range(2):
+            nc.sync.dma_start(w1_raw[:, h], w1v[:, :, h * HALF : (h + 1) * HALF])
         n2_t = load_list("n2_t", n2, 16)
-        w2_raw = sb("w2_raw", [P, 4, S], F32)
-        nc.sync.dma_start(w2_raw[:], w2.rearrange("(p j) c -> p j c", j=4))
         n3_t = load_list("n3_t", n3, 32)
         n4_t = load_list("n4_t", n4, 32)
-        w3w_raw = sb("w3w_raw", [P, 2 * S], U8)
-        nc.sync.dma_start(w3w_raw[:].bitcast(I32), w3_words[0].bitcast(I32))
-        load_scale_rows(nc.sync, w3s_raw, w3_scales)
-        res_t = sb("res_t", [P, 4, S], F32)
-        nc.sync.dma_start(res_t[:], res.rearrange("(p t) c -> p t c", t=4))
 
-        xgs = sb("xgs", [P, S], U8)
-        nc.vector.tensor_copy(xgs[:], xs[:].indirect(offs_t[:]))
         xg = sb("xg", [P, S], U32)
         nc.vector.tensor_copy(xg[:], xw[:].indirect(offs_t[:]))
+        xgs = sb("xgs", [P, S], U8)
+        nc.vector.tensor_copy(xgs[:], xs[:].indirect(offs_t[:]))
 
         w1b = sb("w1b", [P, 4, P, 4], BF16)
         for h, m0, m1, copy in (
@@ -94,13 +86,21 @@ def tile_picked_deepfillrange_none_po_kernel(
         ):
             copy(
                 w1b[:, :, 64 * h + m0 : 64 * h + m1, :].rearrange("p t m j -> p m t j"),
-                w1_raw[h][:, :, 4 * m0 : 4 * m1].rearrange("p j (m t) -> p m t j", t=4),
+                w1_raw[:, h, :, 4 * m0 : 4 * m1].rearrange("p j (m t) -> p m t j", t=4),
             )
         w1q = sb("w1q", [P, S], U32)
         w1s = sb("w1s", [P, S], U8)
         w1f = w1b[:].rearrange("p t m j -> p (t m j)")
         for a, b in ((0, 128), (128, 256), (256, 512)):
             nc.vector.quantize_mx(out=w1q[:, a:b].bitcast(FP8X4), scales=w1s[:, a:b], in_=w1f[:, 4 * a : 4 * b])
+
+        w2_raw = sb("w2_raw", [P, 4, S], F32, tag="w1_raw")
+        nc.sync.dma_start(w2_raw[:], w2.rearrange("(p j) c -> p j c", j=4))
+        res_t = sb("res_t", [P, 4, S], F32, tag="xw")
+        nc.sync.dma_start(res_t[:], res.rearrange("(p t) c -> p t c", t=4))
+        w3w_raw = sb("w3w_raw", [P, 2 * S], U8, tag="w1b")
+        nc.sync.dma_start(w3w_raw[:].bitcast(I32), w3_words[0].bitcast(I32))
+        load_scale_rows(nc.sync, w3s_raw, w3_scales)
 
         zc = sb("zc", [P, 4, S], BF16)
         for t in range(4):
@@ -142,25 +142,27 @@ def tile_picked_deepfillrange_none_po_kernel(
 
         zb = [sb("zb%d" % h, [P, HALF, 4], BF16) for h in range(2)]
         interleave(nc.vector.tensor_copy, zb[0][:], zc[:, :, 0:256])
-        interleave(nc.scalar.copy, zb[1][:, 0:128, :], zc[:, :, 256:384])
-        interleave(nc.vector.tensor_copy, zb[1][:, 128:256, :], zc[:, :, 384:512])
+        interleave(nc.scalar.copy, zb[1][:, 0:192, :], zc[:, :, 256:448])
+        interleave(nc.vector.tensor_copy, zb[1][:, 192:256, :], zc[:, :, 448:512])
         hw = [sb("hw%d" % t, [P, S], F32) for t in range(4)]
         ha = sb("ha", [P, 4, S], F32)
-        zq = [sb("zq%d" % h, [P, HALF], U32) for h in range(2)]
-        zs = [sb("zs%d" % h, [P, HALF], U8) for h in range(2)]
+        zq = sb("zq", [P, S], U32)
+        zs = sb("zs", [P, S], U8)
         for h in range(2):
+            part = slice(h * HALF, (h + 1) * HALF)
             nc.vector.quantize_mx(
-                out=zq[h][:].bitcast(FP8X4), scales=zs[h][:], in_=zb[h][:].rearrange("p c t -> p (c t)")
+                out=zq[:, part].bitcast(FP8X4), scales=zs[:, part], in_=zb[h][:].rearrange("p c t -> p (c t)")
             )
         for t in range(4):
             cols = slice(t * P, (t + 1) * P)
-            for h in range(2):
-                acc = bank(4 * h + t, "h_acc%d_%d" % (h, t))
+            parts = ((0, 0, HALF), (4, HALF, S)) if t == 0 else ((t, 0, S),)
+            for b, c0, c1 in parts:
+                acc = bank(b, "h_acc%d_%d" % (t, c0))
                 nc.tensor.matmul_mx(
-                    out=acc[:, 0:HALF], lhsT=w2q[:, cols].bitcast(FP8X4), lhsT_scale=w2s[:, cols],
-                    rhs=zq[h][:].bitcast(FP8X4), rhs_scale=zs[h][:], start=True, stop=True,
+                    out=acc[:, 0 : c1 - c0], lhsT=w2q[:, cols].bitcast(FP8X4), lhsT_scale=w2s[:, cols],
+                    rhs=zq[:, c0:c1].bitcast(FP8X4), rhs_scale=zs[:, c0:c1], start=True, stop=True,
                 )
-                nc.scalar.copy(hw[t][:, h * HALF : (h + 1) * HALF], acc[:, 0:HALF])
+                nc.scalar.copy(hw[t][:, c0:c1], acc[:, 0 : c1 - c0])
             nc.scalar.copy(ha[:, t, 0:NC], hw[t][:, 0:NC])
 
         w3w = sb("w3w", [P, 2 * S], U8, tag="zb1")
@@ -174,71 +176,93 @@ def tile_picked_deepfillrange_none_po_kernel(
         osc = sb("osc", [P, S], U8)
         out0v = out_0.rearrange("(p t) c -> p t c", t=4)
         out1v = out_1[0].rearrange("p c r -> p (c r)").bitcast(I32)
-        n = NC
-        for c in range(4):
-            lists = slice(8 * c, 8 * c + 8)
-            cols = slice(c * n, (c + 1) * n)
-            d1 = sb("d1_%d" % c, [P, 4, n], F32)
-            d2 = sb("d2_%d" % c, [P, 4, n], F32)
-            neg = sb("neg%d" % c, [P, 4, n], F32)
-            up = sb("up%d" % c, [P, 4, n], F32)
-            down = sb("down%d" % c, [P, 4, n], F32)
-            half = sb("half%d" % c, [P, 4, n], F32)
+        accs = []
+        for c0, n in STRETCHES:
+            lists = slice(c0 // 16, (c0 + n) // 16)
+            cols = slice(c0, c0 + n)
+            d1 = sb("d1_%d" % c0, [P, 4, n], F32, tag="ring%d" % (c0 // NC % 2))
+            d2 = sb("d2_%d" % c0, [P, 4, n], F32)
+            neg = sb("neg%d" % c0, [P, 4, n], F32)
+            up = sb("up%d" % c0, [P, 4, n], F32)
+            down = sb("down%d" % c0, [P, 4, n], F32)
+            half = sb("half%d" % c0, [P, 4, n], F32)
             for t in range(4):
                 nc.vector.tensor_tensor(d1[:, t, :], hw[t][:].indirect(n3_t[:, lists]), ha[:, t, cols], ALU.subtract)
                 nc.vector.tensor_tensor(d2[:, t, :], hw[t][:].indirect(n4_t[:, lists]), ha[:, t, cols], ALU.subtract)
                 if t % 2:
                     ts = slice(t - 1, t + 1)
                     nc.scalar.activation(neg[:, ts, :], d1[:, ts, :], ACT.Relu, scale=-0.5)
-            if c == 0:
+            if c0 == 0:
                 for t in range(4):
                     nc.scalar.copy(ha[:, t, NC:S], hw[t][:, NC:S])
             nc.scalar.activation(half[:], ha[:, :, cols], ACT.Copy, scale=0.5)
-            sum_t = bank(3 * (c % 2), "sum_t%d" % c)
-            for t in range(4):
-                nc.tensor.matmul(
-                    sum_t[:, t * P : (t + 1) * P], half[:, t, :], ident[:], is_transpose=True, start=(t == 0), stop=False
-                )
             for g in range(2):
                 ts = slice(2 * g, 2 * g + 2)
                 nc.vector.scalar_tensor_tensor(up[:, ts, :], d1[:, ts, :], 0.0, d2[:, ts, :], ALU.max, ALU.max)
                 nc.vector.scalar_tensor_tensor(down[:, ts, :], d2[:, ts, :], -0.5, neg[:, ts, :], ALU.mult, ALU.max)
-                for term in (up, down):
-                    for t in (2 * g, 2 * g + 1):
+            for s0 in range(0, n, NC):
+                c = (c0 + s0) // NC
+                sub = slice(s0, s0 + NC)
+                pairs = sb("pairs%d" % c, [P, 2, P, 2], BF16)
+                words = pairs[:].rearrange("j u p e -> j (u p e)").bitcast(F32)
+                back = bank(2 + c % 2, "back%d" % c)
+                for u in range(2):
+                    sum_t = bank(u, "sum_t%d_%d" % (c, u))
+                    order = [(term, e) for term in (half, up, down) for e in range(2)]
+                    for k, (term, e) in enumerate(order):
                         nc.tensor.matmul(
-                            sum_t[:, t * P : (t + 1) * P], term[:, t, :], ident[:], is_transpose=True,
-                            start=False, stop=(term is down and t == 3),
+                            sum_t[:, e * P : (e + 1) * P], term[:, 2 * u + e, sub], ident[:], is_transpose=True,
+                            start=(k == 0), stop=(k == len(order) - 1),
                         )
-            pairs = sb("pairs%d" % c, [P, 2, P, 2], BF16)
-            nc.scalar.copy(pairs[:], sum_t[:].rearrange("j (u e p) -> j u p e", u=2, e=2))
-            back = bank(3 * (c % 2) + 1, "back%d" % c)
-            words = pairs[:].rearrange("j u p e -> j (u p e)").bitcast(F32)
-            for u in range(2):
-                nc.tensor.transpose(back[:, u * P : (u + 1) * P], words[:, u * P : (u + 1) * P], ident[:])
-            z2b = sb("z2b%d" % c, [P, 4 * n], BF16)
-            nc.scalar.copy(
-                z2b[:].bitcast(F32).rearrange("p (j u) -> p j u", u=2),
-                back[:, 0 : 2 * P].rearrange("p (u j) -> p j u", u=2),
-            )
-            z2q = sb("z2q%d" % c, [P, n], U32)
-            z2s = sb("z2s%d" % c, [P, n], U8)
-            nc.vector.quantize_mx(out=z2q[:].bitcast(FP8X4), scales=z2s[:], in_=z2b[:])
-            o = sb("o%d" % c, [P, 4, n], F32)
-            acc = bank(3 * (c % 2) + 2, "o_acc%d" % c)
-            for t in range(4):
-                nc.tensor.matmul_mx(
-                    out=acc[:, t * n : (t + 1) * n],
-                    lhsT=w3w[:, 256 * t : 256 * (t + 1)].bitcast(FP4X4), lhsT_scale=w3s[:, t * P : (t + 1) * P],
-                    rhs=z2q[:].bitcast(FP8X4), rhs_scale=z2s[:], start=True, stop=True,
+                    nc.scalar.copy(pairs[:, u], sum_t[:, 0 : 2 * P].rearrange("j (e p) -> j p e", e=2))
+                    nc.tensor.transpose(back[:, u * P : (u + 1) * P], words[:, u * P : (u + 1) * P], ident[:])
+                z2b = sb("z2b%d" % c, [P, 4 * NC], BF16, tag="ring%d" % (c % 2))
+                nc.scalar.copy(
+                    z2b[:].bitcast(F32).rearrange("p (j u) -> p j u", u=2),
+                    back[:, 0 : 2 * P].rearrange("p (u j) -> p j u", u=2),
                 )
-            nc.vector.tensor_tensor(o[:], acc[:].rearrange("p (k n) -> p k n", n=n), res_t[:, :, cols], ALU.add)
+                z2q = sb("z2q%d" % c, [P, NC], U32)
+                z2s = sb("z2s%d" % c, [P, NC], U8)
+                nc.vector.quantize_mx(out=z2q[:].bitcast(FP8X4), scales=z2s[:], in_=z2b[:])
+                acc = bank(4 + c, "o_acc%d" % c)
+                for t in range(4):
+                    nc.tensor.matmul_mx(
+                        out=acc[:, t * NC : (t + 1) * NC],
+                        lhsT=w3w[:, 256 * t : 256 * (t + 1)].bitcast(FP4X4), lhsT_scale=w3s[:, t * P : (t + 1) * P],
+                        rhs=z2q[:].bitcast(FP8X4), rhs_scale=z2s[:], start=True, stop=True,
+                    )
+                accs.append(acc)
+        outs = {}
+
+        def add_residual(c, tag):
+            cols = slice(c * NC, (c + 1) * NC)
+            o = sb("o%d" % c, [P, 4, NC], F32, tag=tag)
+            nc.vector.tensor_tensor(o[:], accs[c][:].rearrange("p (k n) -> p k n", n=NC), res_t[:, :, cols], ALU.add)
             nc.sync.dma_start(out0v[:, :, cols], o[:])
-            ob = sb("ob%d" % c, [P, n, 4], BF16)
-            interleave(nc.scalar.copy, ob[:], o[:])
+            outs[c] = o
+
+        ob = sb("ob", [P, S * 4], BF16, tag="pairs3")
+
+        def round_out(c, copy):
+            interleave(copy, ob[:, 4 * NC * c : 4 * NC * (c + 1)].rearrange("p (c t) -> p c t", t=4), outs[c][:])
+
+        def planes(c0, c1):
+            cols = slice(c0 * NC, c1 * NC)
             nc.vector.quantize_mx(
-                out=oq[:, cols].bitcast(FP8X4), scales=osc[:, cols], in_=ob[:].rearrange("p c t -> p (c t)")
+                out=oq[:, cols].bitcast(FP8X4), scales=osc[:, cols], in_=ob[:, 4 * NC * c0 : 4 * NC * c1]
             )
             nc.sync.dma_start(out1v[:, cols], oq[:, cols].bitcast(I32))
+
+        add_residual(0, "neg384")
+        add_residual(1, "d2_384")
+        add_residual(2, None)
+        add_residual(3, None)
+        round_out(3, nc.vector.tensor_copy)
+        planes(3, 4)
+        for c in range(3):
+            round_out(c, nc.scalar.copy)
+        planes(0, 2)
+        planes(2, 3)
         for q in range(4):
             eng = nc.scalar if q % 2 else nc.sync
             eng.dma_start(out_2[0, 4 * q : 4 * q + 4, :].bitcast(I32), osc[32 * q : 32 * q + 4, :].bitcast(I32))

@@ -21,7 +21,7 @@ W = 256
 HALF = 256
 NC = 128
 STRETCHES = ((0, 128), (128, 128), (256, 128), (384, 128))
-W1_SPLIT = 40
+W1_SPLIT = 44
 
 FLOPS = 805306368
 
@@ -53,34 +53,39 @@ def tile_picked_deepfillrange_none_po_kernel(
             copy(dst.rearrange("p (c i) t -> p c t i", i=4), src.rearrange("p t (c i) -> p c t i", i=4))
 
         xs = sb("xs", [P, T], U8)
-        nc.vector.memset(xs[:].bitcast(I32), 0)
+        for p0, p1 in ((0, 16), (32, 64), (64, 128)):
+            nc.vector.memset(xs[p0:p1, :].bitcast(I32), 0)
+        xgs = sb("xgs", [P, S], U8)
+        nc.gpsimd.memset(xgs[:].bitcast(I32), 0)
         ident = sb("ident", [P, P], F32)
         make_identity(nc, ident[:])
 
-        w3s_raw = sb("w3s_raw", [P, S], U8)
-        nc.gpsimd.memset(w3s_raw[:].bitcast(I32), 0)
 
         offs_t = load_list("offs_t", offs, 32)
+        nc.sync.dma_start(xs[16:32, :].bitcast(I32), x_scales[0].bitcast(I32))
         xw = sb("xw", [P, T], U32)
         nc.sync.dma_start(xw[:].bitcast(I32), x_words[0].rearrange("p c r -> p (c r)").bitcast(I32))
         n1_t = load_list("n1_t", n1, 16)
-        load_scale_rows(nc.sync, xs, x_scales)
+        n2_t = load_list("n2_t", n2, 16)
+        n3_t = load_list("n3_t", n3, 32)
+        n4_t = load_list("n4_t", n4, 32)
         w1v = w1.rearrange("(p j) c -> p j c", j=4)
         w1_raw = sb("w1_raw", [P, 2, 4, HALF], F32)
         for h in range(2):
             nc.sync.dma_start(w1_raw[:, h], w1v[:, :, h * HALF : (h + 1) * HALF])
-        n2_t = load_list("n2_t", n2, 16)
-        n3_t = load_list("n3_t", n3, 32)
-        n4_t = load_list("n4_t", n4, 32)
 
+        picked_rows = sb("picked_rows", [P, S], U8)
+        nc.vector.tensor_copy(picked_rows[:], xs[:].indirect(offs_t[:]))
+        for q in range(4):
+            nc.scalar.dma_start(
+                xgs[32 * q : 32 * q + 4, :].bitcast(I32), picked_rows[16 + 4 * q : 20 + 4 * q, :].bitcast(I32)
+            )
         xg = sb("xg", [P, S], U32)
         nc.vector.tensor_copy(xg[:], xw[:].indirect(offs_t[:]))
-        xgs = sb("xgs", [P, S], U8)
-        nc.vector.tensor_copy(xgs[:], xs[:].indirect(offs_t[:]))
 
         w1b = sb("w1b", [P, 4, P, 4], BF16)
         for h, m0, m1, copy in (
-            (0, 0, 64, nc.scalar.copy),
+            (0, 0, 64, nc.vector.tensor_copy),
             (1, 0, W1_SPLIT, nc.vector.tensor_copy),
             (1, W1_SPLIT, 64, nc.scalar.copy),
         ):
@@ -96,13 +101,20 @@ def tile_picked_deepfillrange_none_po_kernel(
 
         w2_raw = sb("w2_raw", [P, 4, S], F32, tag="w1_raw")
         nc.sync.dma_start(w2_raw[:], w2.rearrange("(p j) c -> p j c", j=4))
-        res_t = sb("res_t", [P, 4, S], F32, tag="xw")
-        nc.sync.dma_start(res_t[:], res.rearrange("(p t) c -> p t c", t=4))
         w3w_raw = sb("w3w_raw", [P, 2 * S], U8, tag="w1b")
         nc.sync.dma_start(w3w_raw[:].bitcast(I32), w3_words[0].bitcast(I32))
-        load_scale_rows(nc.sync, w3s_raw, w3_scales)
 
-        zc = sb("zc", [P, 4, S], BF16)
+        w2b = sb("w2b", [P, 4, P, 4], BF16)
+        for k in range(4):
+            nc.scalar.copy(
+                w2b[:, :, 32 * k : 32 * k + 32, :].rearrange("p t m j -> p m t j"),
+                w2_raw[:, :, 128 * k : 128 * k + 128].rearrange("p j (m t) -> p m t j", t=4),
+            )
+
+        res_t = sb("res_t", [P, 4, S], F32, tag="w1_raw")
+        nc.sync.dma_start(res_t[:], res.rearrange("(p t) c -> p t c", t=4))
+
+        ys = []
         for t in range(4):
             cols = slice(t * P, (t + 1) * P)
             y = sb("y%d" % t, [P, S], F32)
@@ -127,15 +139,16 @@ def tile_picked_deepfillrange_none_po_kernel(
                 nc.vector.tensor_tensor(d[:, part], y[:].indirect(n2_t[:, 8 * k : 8 * k + 8]), pa[:, part], ALU.subtract)
             nc.scalar.activation(r[:], d[:], ACT.Relu)
             nc.vector.tensor_tensor(y[:].indirect(n1_t[:]), pa[:], r[:], ALU.add)
-            for h in range(2):
-                nc.scalar.copy(zc[:, t, h * HALF : (h + 1) * HALF], y[:, h * HALF : (h + 1) * HALF])
+            ys.append(y)
+        w3s_raw = sb("w3s_raw", [P, S], U8, tag="xg")
+        nc.gpsimd.memset(w3s_raw[:].bitcast(I32), 0)
+        load_scale_rows(nc.sync, w3s_raw, w3_scales)
+        zc = sb("zc", [P, 4, S], BF16, tag="d3")
+        for t in range(3):
+            nc.scalar.copy(zc[:, t, :], ys[t][:])
+        for h in range(2):
+            nc.scalar.copy(zc[:, 3, h * HALF : (h + 1) * HALF], ys[3][:, h * HALF : (h + 1) * HALF])
 
-        w2b = sb("w2b", [P, 4, P, 4], BF16)
-        for k in range(4):
-            nc.scalar.copy(
-                w2b[:, :, 32 * k : 32 * k + 32, :].rearrange("p t m j -> p m t j"),
-                w2_raw[:, :, 128 * k : 128 * k + 128].rearrange("p j (m t) -> p m t j", t=4),
-            )
         w2q = sb("w2q", [P, S], U32, tag="pa3")
         w2s = sb("w2s", [P, S], U8)
         nc.vector.quantize_mx(out=w2q[:].bitcast(FP8X4), scales=w2s[:], in_=w2b[:].rearrange("p t m j -> p (t m j)"))
@@ -163,13 +176,15 @@ def tile_picked_deepfillrange_none_po_kernel(
                     rhs=zq[:, c0:c1].bitcast(FP8X4), rhs_scale=zs[:, c0:c1], start=True, stop=True,
                 )
                 nc.scalar.copy(hw[t][:, c0:c1], acc[:, 0 : c1 - c0])
-            nc.scalar.copy(ha[:, t, 0:NC], hw[t][:, 0:NC])
+                if c0 == 0:
+                    nc.scalar.copy(ha[:, t, 0:NC], acc[:, 0:NC])
+            nc.sync.dma_start(ha[:, t, NC:S], hw[t][:, NC:S])
 
         w3w = sb("w3w", [P, 2 * S], U8, tag="zb1")
         nc.vector.tensor_copy(
             w3w[:].rearrange("p (t m e) -> p m t e", t=4, e=2), w3w_raw[:].rearrange("p (m t e) -> p m t e", t=4, e=2)
         )
-        w3s = sb("w3s", [P, S], U8, tag="zb0")
+        w3s = sb("w3s", [P, S], U8, tag="d3")
         nc.vector.tensor_copy(w3s[:].rearrange("p (t m) -> p m t", t=4), w3s_raw[:].rearrange("p (m t) -> p m t", t=4))
 
         oq = sb("oq", [P, S], U32)
@@ -180,21 +195,18 @@ def tile_picked_deepfillrange_none_po_kernel(
         for c0, n in STRETCHES:
             lists = slice(c0 // 16, (c0 + n) // 16)
             cols = slice(c0, c0 + n)
-            d1 = sb("d1_%d" % c0, [P, 4, n], F32, tag="ring%d" % (c0 // NC % 2))
-            d2 = sb("d2_%d" % c0, [P, 4, n], F32)
-            neg = sb("neg%d" % c0, [P, 4, n], F32)
-            up = sb("up%d" % c0, [P, 4, n], F32)
+            d1 = sb("d1_%d" % c0, [P, 4, n], F32, tag="d1")
+            d2 = sb("d2_%d" % c0, [P, 4, n], F32, tag="d2")
+            neg = sb("neg%d" % c0, [P, 4, n], F32, tag="pairs%d" % (c0 // NC - 1) if c0 else None)
+            up = sb("up%d" % c0, [P, 4, n], F32, tag="z2b2" if c0 == 384 else None)
             down = sb("down%d" % c0, [P, 4, n], F32)
-            half = sb("half%d" % c0, [P, 4, n], F32)
+            half = sb("half%d" % c0, [P, 4, n], F32, tag="down%d" % (c0 - NC) if c0 else None)
             for t in range(4):
                 nc.vector.tensor_tensor(d1[:, t, :], hw[t][:].indirect(n3_t[:, lists]), ha[:, t, cols], ALU.subtract)
                 nc.vector.tensor_tensor(d2[:, t, :], hw[t][:].indirect(n4_t[:, lists]), ha[:, t, cols], ALU.subtract)
                 if t % 2:
                     ts = slice(t - 1, t + 1)
                     nc.scalar.activation(neg[:, ts, :], d1[:, ts, :], ACT.Relu, scale=-0.5)
-            if c0 == 0:
-                for t in range(4):
-                    nc.scalar.copy(ha[:, t, NC:S], hw[t][:, NC:S])
             nc.scalar.activation(half[:], ha[:, :, cols], ACT.Copy, scale=0.5)
             for g in range(2):
                 ts = slice(2 * g, 2 * g + 2)
@@ -216,7 +228,7 @@ def tile_picked_deepfillrange_none_po_kernel(
                         )
                     nc.scalar.copy(pairs[:, u], sum_t[:, 0 : 2 * P].rearrange("j (e p) -> j p e", e=2))
                     nc.tensor.transpose(back[:, u * P : (u + 1) * P], words[:, u * P : (u + 1) * P], ident[:])
-                z2b = sb("z2b%d" % c, [P, 4 * NC], BF16, tag="ring%d" % (c % 2))
+                z2b = sb("z2b%d" % c, [P, 4 * NC], BF16)
                 nc.scalar.copy(
                     z2b[:].bitcast(F32).rearrange("p (j u) -> p j u", u=2),
                     back[:, 0 : 2 * P].rearrange("p (u j) -> p j u", u=2),
@@ -224,20 +236,25 @@ def tile_picked_deepfillrange_none_po_kernel(
                 z2q = sb("z2q%d" % c, [P, NC], U32)
                 z2s = sb("z2s%d" % c, [P, NC], U8)
                 nc.vector.quantize_mx(out=z2q[:].bitcast(FP8X4), scales=z2s[:], in_=z2b[:])
-                acc = bank(4 + c, "o_acc%d" % c)
-                for t in range(4):
-                    nc.tensor.matmul_mx(
-                        out=acc[:, t * NC : (t + 1) * NC],
-                        lhsT=w3w[:, 256 * t : 256 * (t + 1)].bitcast(FP4X4), lhsT_scale=w3s[:, t * P : (t + 1) * P],
-                        rhs=z2q[:].bitcast(FP8X4), rhs_scale=z2s[:], start=True, stop=True,
-                    )
-                accs.append(acc)
+                groups = ((4 + c, 0, 2), (0, 2, 4)) if c == 3 else ((4 + c, 0, 4),)
+                accs.append([])
+                for b, t0, t1 in groups:
+                    acc = bank(b, "o_acc%d_%d" % (c, t0))
+                    for t in range(t0, t1):
+                        nc.tensor.matmul_mx(
+                            out=acc[:, (t - t0) * NC : (t - t0 + 1) * NC],
+                            lhsT=w3w[:, 256 * t : 256 * (t + 1)].bitcast(FP4X4), lhsT_scale=w3s[:, t * P : (t + 1) * P],
+                            rhs=z2q[:].bitcast(FP8X4), rhs_scale=z2s[:], start=True, stop=True,
+                        )
+                    accs[c].append((acc, t0, t1))
         outs = {}
 
         def add_residual(c, tag):
             cols = slice(c * NC, (c + 1) * NC)
             o = sb("o%d" % c, [P, 4, NC], F32, tag=tag)
-            nc.vector.tensor_tensor(o[:], accs[c][:].rearrange("p (k n) -> p k n", n=NC), res_t[:, :, cols], ALU.add)
+            for acc, t0, t1 in accs[c]:
+                sums = acc[:, 0 : (t1 - t0) * NC].rearrange("p (k n) -> p k n", n=NC)
+                nc.vector.tensor_tensor(o[:, t0:t1, :], sums, res_t[:, t0:t1, cols], ALU.add)
             nc.sync.dma_start(out0v[:, :, cols], o[:])
             outs[c] = o
 
@@ -253,14 +270,15 @@ def tile_picked_deepfillrange_none_po_kernel(
             )
             nc.sync.dma_start(out1v[:, cols], oq[:, cols].bitcast(I32))
 
-        add_residual(0, "neg384")
-        add_residual(1, "d2_384")
-        add_residual(2, None)
+        add_residual(0, "pairs2")
+        add_residual(1, "d2")
+        add_residual(2, "down384")
         add_residual(3, None)
         round_out(3, nc.vector.tensor_copy)
         planes(3, 4)
-        for c in range(3):
-            round_out(c, nc.scalar.copy)
+        round_out(0, nc.vector.tensor_copy)
+        round_out(1, nc.scalar.copy)
+        round_out(2, nc.scalar.copy)
         planes(0, 2)
         planes(2, 3)
         for q in range(4):

@@ -15,13 +15,21 @@ ALU = mybir.AluOpType
 ACT = mybir.ActivationFunctionType
 
 P = 128
-T = 2048
+PLANES = 4
+TOKENS = 2048
 S = 512
-W = 256
-HALF = 256
-NC = 128
-STRETCHES = ((0, 128), (128, 128), (256, 128), (384, 128))
-W1_SPLIT = 44
+PAIRS = 256
+HALF = S // 2
+CHUNK = 128
+CHUNKS = S // CHUNK
+LAST = CHUNKS - 1
+PER_COLUMN = 16
+SCALE_ROWS = 16
+W1_VECTOR_SHARE = 44
+Z_SCALAR_SHARE = 192
+SPARE_BANK = 4
+OUT_BANK = 4
+BACK_BANK = 2
 
 FLOPS = 805306368
 
@@ -38,249 +46,281 @@ def tile_picked_deepfillrange_none_po_kernel(
             return keep.tile(shape, dtype, name=name, tag=tag or name, align_bytes=64)
 
         def bank(i, name):
-            return psum.tile([P, 512], F32, name=name, tag="bank%d" % i)
+            return psum.tile([P, S], F32, name=name, tag="bank%d" % i)
 
-        def load_list(name, src, cols):
-            t = keep.tile([P, cols], U16, name=name)
-            nc.sync.dma_start(t[:], src)
-            return t
+        def load_list(name, src, entries):
+            lists = keep.tile([P, entries // PER_COLUMN], U16, name=name)
+            nc.sync.dma_start(lists[:], src)
+            return lists
 
-        def load_scale_rows(eng, dst, src):
-            for q in range(4):
-                eng.dma_start(dst[32 * q : 32 * q + 4, :].bitcast(I32), src[0, 4 * q : 4 * q + 4, :].bitcast(I32))
+        def entries_of(lists, c):
+            return lists[:, c * CHUNK // PER_COLUMN : (c + 1) * CHUNK // PER_COLUMN]
 
         def interleave(copy, dst, src):
             copy(dst.rearrange("p (c i) t -> p c t i", i=4), src.rearrange("p t (c i) -> p c t i", i=4))
 
-        xs = sb("xs", [P, T], U8)
-        for p0, p1 in ((0, 16), (32, 64), (64, 128)):
-            nc.vector.memset(xs[p0:p1, :].bitcast(I32), 0)
-        xgs = sb("xgs", [P, S], U8)
-        nc.gpsimd.memset(xgs[:].bitcast(I32), 0)
+        def round_and_deal(copy, dst, src):
+            copy(dst.rearrange("p t m j -> p m t j"), src.rearrange("p j (m t) -> p m t j", t=PLANES))
+
+        def product(acc, weights, weight_scales, codes, scales):
+            nc.tensor.matmul_mx(
+                out=acc, lhsT=weights, lhsT_scale=weight_scales, rhs=codes.bitcast(FP8X4), rhs_scale=scales,
+                start=True, stop=True,
+            )
+
+        def column_parts(t):
+            return ((0, 0, HALF), (SPARE_BANK, HALF, S)) if t == 0 else ((t, 0, S),)
+
+        x_scale_table = sb("x_scale_table", [P, TOKENS], U8)
+        for p0, p1 in ((0, SCALE_ROWS), (32, 64), (64, P)):
+            nc.vector.memset(x_scale_table[p0:p1, :].bitcast(I32), 0)
+        picked_scales = sb("picked_scales", [P, S], U8)
+        nc.gpsimd.memset(picked_scales[:].bitcast(I32), 0)
         ident = sb("ident", [P, P], F32)
         make_identity(nc, ident[:])
+        w3_scales_raw = sb("w3_scales_raw", [P, S], U8)
+        nc.gpsimd.memset(w3_scales_raw[:].bitcast(I32), 0)
 
-
-        offs_t = load_list("offs_t", offs, 32)
-        nc.sync.dma_start(xs[16:32, :].bitcast(I32), x_scales[0].bitcast(I32))
-        xw = sb("xw", [P, T], U32)
-        nc.sync.dma_start(xw[:].bitcast(I32), x_words[0].rearrange("p c r -> p (c r)").bitcast(I32))
-        n1_t = load_list("n1_t", n1, 16)
-        n2_t = load_list("n2_t", n2, 16)
-        n3_t = load_list("n3_t", n3, 32)
-        n4_t = load_list("n4_t", n4, 32)
-        w1v = w1.rearrange("(p j) c -> p j c", j=4)
-        w1_raw = sb("w1_raw", [P, 2, 4, HALF], F32)
+        offs_t = load_list("offs_t", offs, S)
+        nc.sync.dma_start(x_scale_table[SCALE_ROWS : 2 * SCALE_ROWS, :].bitcast(I32), x_scales[0].bitcast(I32))
+        x_word_table = sb("x_word_table", [P, TOKENS], U32)
+        nc.sync.dma_start(x_word_table[:].bitcast(I32), x_words[0].rearrange("p c r -> p (c r)").bitcast(I32))
+        w1_rows = w1.rearrange("(p j) c -> p j c", j=PLANES)
+        w1_raw = sb("w1_raw", [P, 2, PLANES, HALF], F32)
         for h in range(2):
-            nc.sync.dma_start(w1_raw[:, h], w1v[:, :, h * HALF : (h + 1) * HALF])
+            nc.sync.dma_start(w1_raw[:, h], w1_rows[:, :, h * HALF : (h + 1) * HALF])
+        n1_t = load_list("n1_t", n1, PAIRS)
+        n2_t = load_list("n2_t", n2, PAIRS)
+        n3_t = load_list("n3_t", n3, S)
+        n4_t = load_list("n4_t", n4, S)
 
         picked_rows = sb("picked_rows", [P, S], U8)
-        nc.vector.tensor_copy(picked_rows[:], xs[:].indirect(offs_t[:]))
+        nc.vector.tensor_copy(picked_rows[:], x_scale_table[:].indirect(offs_t[:]))
         for q in range(4):
             nc.scalar.dma_start(
-                xgs[32 * q : 32 * q + 4, :].bitcast(I32), picked_rows[16 + 4 * q : 20 + 4 * q, :].bitcast(I32)
+                picked_scales[32 * q : 32 * q + 4, :].bitcast(I32),
+                picked_rows[SCALE_ROWS + 4 * q : SCALE_ROWS + 4 * q + 4, :].bitcast(I32),
             )
-        xg = sb("xg", [P, S], U32)
-        nc.vector.tensor_copy(xg[:], xw[:].indirect(offs_t[:]))
+        picked_words = sb("picked_words", [P, S], U32)
+        nc.vector.tensor_copy(picked_words[:], x_word_table[:].indirect(offs_t[:]))
 
-        w1b = sb("w1b", [P, 4, P, 4], BF16)
+        w1_bf = sb("w1_bf", [P, PLANES, P, PLANES], BF16)
+        per_half = HALF // PLANES
         for h, m0, m1, copy in (
-            (0, 0, 64, nc.vector.tensor_copy),
-            (1, 0, W1_SPLIT, nc.vector.tensor_copy),
-            (1, W1_SPLIT, 64, nc.scalar.copy),
+            (0, 0, per_half, nc.vector.tensor_copy),
+            (1, 0, W1_VECTOR_SHARE, nc.vector.tensor_copy),
+            (1, W1_VECTOR_SHARE, per_half, nc.scalar.copy),
         ):
-            copy(
-                w1b[:, :, 64 * h + m0 : 64 * h + m1, :].rearrange("p t m j -> p m t j"),
-                w1_raw[:, h, :, 4 * m0 : 4 * m1].rearrange("p j (m t) -> p m t j", t=4),
+            round_and_deal(
+                copy,
+                w1_bf[:, :, per_half * h + m0 : per_half * h + m1, :],
+                w1_raw[:, h, :, PLANES * m0 : PLANES * m1],
             )
-        w1q = sb("w1q", [P, S], U32)
-        w1s = sb("w1s", [P, S], U8)
-        w1f = w1b[:].rearrange("p t m j -> p (t m j)")
-        for a, b in ((0, 128), (128, 256), (256, 512)):
-            nc.vector.quantize_mx(out=w1q[:, a:b].bitcast(FP8X4), scales=w1s[:, a:b], in_=w1f[:, 4 * a : 4 * b])
+        w1_codes = sb("w1_codes", [P, S], U32)
+        w1_scales = sb("w1_scales", [P, S], U8)
+        w1_flat = w1_bf[:].rearrange("p t m j -> p (t m j)")
+        for t0, t1 in ((0, 1), (1, 2), (2, PLANES)):
+            nc.vector.quantize_mx(
+                out=w1_codes[:, P * t0 : P * t1].bitcast(FP8X4),
+                scales=w1_scales[:, P * t0 : P * t1],
+                in_=w1_flat[:, S * t0 : S * t1],
+            )
 
-        w2_raw = sb("w2_raw", [P, 4, S], F32, tag="w1_raw")
-        nc.sync.dma_start(w2_raw[:], w2.rearrange("(p j) c -> p j c", j=4))
-        w3w_raw = sb("w3w_raw", [P, 2 * S], U8, tag="w1b")
-        nc.sync.dma_start(w3w_raw[:].bitcast(I32), w3_words[0].bitcast(I32))
-
-        w2b = sb("w2b", [P, 4, P, 4], BF16)
+        w2_raw = sb("w2_raw", [P, PLANES, S], F32, tag="w1_raw")
+        nc.sync.dma_start(w2_raw[:], w2.rearrange("(p j) c -> p j c", j=PLANES))
+        w3_words_raw = sb("w3_words_raw", [P, 2 * S], U8, tag="w1_bf")
+        nc.sync.dma_start(w3_words_raw[:].bitcast(I32), w3_words[0].bitcast(I32))
+        for q in range(4):
+            nc.sync.dma_start(
+                w3_scales_raw[32 * q : 32 * q + 4, :].bitcast(I32), w3_scales[0, 4 * q : 4 * q + 4, :].bitcast(I32)
+            )
+        w2_bf = sb("w2_bf", [P, PLANES, P, PLANES], BF16)
+        per_piece = P // 4
         for k in range(4):
-            nc.scalar.copy(
-                w2b[:, :, 32 * k : 32 * k + 32, :].rearrange("p t m j -> p m t j"),
-                w2_raw[:, :, 128 * k : 128 * k + 128].rearrange("p j (m t) -> p m t j", t=4),
+            round_and_deal(
+                nc.scalar.copy,
+                w2_bf[:, :, per_piece * k : per_piece * (k + 1), :],
+                w2_raw[:, :, PLANES * per_piece * k : PLANES * per_piece * (k + 1)],
             )
+        res_t = sb("res_t", [P, PLANES, S], F32, tag="w1_raw")
+        nc.sync.dma_start(res_t[:], res.rearrange("(p t) c -> p t c", t=PLANES))
 
-        res_t = sb("res_t", [P, 4, S], F32, tag="w1_raw")
-        nc.sync.dma_start(res_t[:], res.rearrange("(p t) c -> p t c", t=4))
-
-        ys = []
-        for t in range(4):
-            cols = slice(t * P, (t + 1) * P)
+        z_planes = []
+        for t in range(PLANES):
+            places = slice(t * P, (t + 1) * P)
             y = sb("y%d" % t, [P, S], F32)
-            if t == 0:
-                parts = ((0, 0, HALF, nc.scalar.copy), (4, HALF, S, nc.vector.tensor_copy))
-            else:
-                parts = ((t, 0, S, nc.scalar.copy),)
-            for b, c0, c1, copy in parts:
+            for b, c0, c1 in column_parts(t):
                 acc = bank(b, "y_acc%d_%d" % (t, c0))
-                nc.tensor.matmul_mx(
-                    out=acc[:, 0 : c1 - c0], lhsT=w1q[:, cols].bitcast(FP8X4), lhsT_scale=w1s[:, cols],
-                    rhs=xg[:, c0:c1].bitcast(FP8X4), rhs_scale=xgs[:, c0:c1], start=True, stop=True,
+                product(
+                    acc[:, 0 : c1 - c0], w1_codes[:, places].bitcast(FP8X4), w1_scales[:, places],
+                    picked_words[:, c0:c1], picked_scales[:, c0:c1],
                 )
+                copy = nc.vector.tensor_copy if b == SPARE_BANK else nc.scalar.copy
                 copy(y[:, c0:c1], acc[:, 0 : c1 - c0])
-            pa = sb("pa%d" % t, [P, W], F32)
-            d = sb("d%d" % t, [P, W], F32)
-            r = sb("r%d" % t, [P, W], F32)
+            pa = sb("pa%d" % t, [P, PAIRS], F32)
+            gap = sb("gap%d" % t, [P, PAIRS], F32)
+            rise = sb("rise%d" % t, [P, PAIRS], F32)
             for k in range(2):
-                nc.vector.tensor_copy(pa[:, k * NC : (k + 1) * NC], y[:].indirect(n1_t[:, 8 * k : 8 * k + 8]))
+                nc.vector.tensor_copy(pa[:, k * CHUNK : (k + 1) * CHUNK], y[:].indirect(entries_of(n1_t, k)))
             for k in range(2):
-                part = slice(k * NC, (k + 1) * NC)
-                nc.vector.tensor_tensor(d[:, part], y[:].indirect(n2_t[:, 8 * k : 8 * k + 8]), pa[:, part], ALU.subtract)
-            nc.scalar.activation(r[:], d[:], ACT.Relu)
-            nc.vector.tensor_tensor(y[:].indirect(n1_t[:]), pa[:], r[:], ALU.add)
-            ys.append(y)
-        w3s_raw = sb("w3s_raw", [P, S], U8, tag="xg")
-        nc.gpsimd.memset(w3s_raw[:].bitcast(I32), 0)
-        load_scale_rows(nc.sync, w3s_raw, w3_scales)
-        zc = sb("zc", [P, 4, S], BF16, tag="d3")
-        for t in range(3):
-            nc.scalar.copy(zc[:, t, :], ys[t][:])
+                part = slice(k * CHUNK, (k + 1) * CHUNK)
+                nc.vector.tensor_tensor(gap[:, part], y[:].indirect(entries_of(n2_t, k)), pa[:, part], ALU.subtract)
+            nc.scalar.activation(rise[:], gap[:], ACT.Relu)
+            nc.vector.tensor_tensor(y[:].indirect(n1_t[:]), pa[:], rise[:], ALU.add)
+            z_planes.append(y)
+
+        z_bf = sb("z_bf", [P, PLANES, S], BF16, tag="gap3")
+        for t in range(PLANES - 1):
+            nc.scalar.copy(z_bf[:, t, :], z_planes[t][:])
         for h in range(2):
-            nc.scalar.copy(zc[:, 3, h * HALF : (h + 1) * HALF], ys[3][:, h * HALF : (h + 1) * HALF])
+            part = slice(h * HALF, (h + 1) * HALF)
+            nc.scalar.copy(z_bf[:, PLANES - 1, part], z_planes[PLANES - 1][:, part])
 
-        w2q = sb("w2q", [P, S], U32, tag="pa3")
-        w2s = sb("w2s", [P, S], U8)
-        nc.vector.quantize_mx(out=w2q[:].bitcast(FP8X4), scales=w2s[:], in_=w2b[:].rearrange("p t m j -> p (t m j)"))
+        w2_codes = sb("w2_codes", [P, S], U32, tag="pa3")
+        w2_scales = sb("w2_scales", [P, S], U8)
+        nc.vector.quantize_mx(
+            out=w2_codes[:].bitcast(FP8X4), scales=w2_scales[:], in_=w2_bf[:].rearrange("p t m j -> p (t m j)")
+        )
 
-        zb = [sb("zb%d" % h, [P, HALF, 4], BF16) for h in range(2)]
-        interleave(nc.vector.tensor_copy, zb[0][:], zc[:, :, 0:256])
-        interleave(nc.scalar.copy, zb[1][:, 0:192, :], zc[:, :, 256:448])
-        interleave(nc.vector.tensor_copy, zb[1][:, 192:256, :], zc[:, :, 448:512])
-        hw = [sb("hw%d" % t, [P, S], F32) for t in range(4)]
-        ha = sb("ha", [P, 4, S], F32)
-        zq = sb("zq", [P, S], U32)
-        zs = sb("zs", [P, S], U8)
+        z_woven = [sb("z_woven%d" % h, [P, HALF, PLANES], BF16) for h in range(2)]
+        interleave(nc.vector.tensor_copy, z_woven[0][:], z_bf[:, :, 0:HALF])
+        interleave(nc.scalar.copy, z_woven[1][:, 0:Z_SCALAR_SHARE, :], z_bf[:, :, HALF : HALF + Z_SCALAR_SHARE])
+        interleave(nc.vector.tensor_copy, z_woven[1][:, Z_SCALAR_SHARE:HALF, :], z_bf[:, :, HALF + Z_SCALAR_SHARE : S])
+        h_table = [sb("h_table%d" % t, [P, S], F32) for t in range(PLANES)]
+        h_plain = sb("h_plain", [P, PLANES, S], F32)
+        z_codes = sb("z_codes", [P, S], U32)
+        z_scales = sb("z_scales", [P, S], U8)
         for h in range(2):
             part = slice(h * HALF, (h + 1) * HALF)
             nc.vector.quantize_mx(
-                out=zq[:, part].bitcast(FP8X4), scales=zs[:, part], in_=zb[h][:].rearrange("p c t -> p (c t)")
+                out=z_codes[:, part].bitcast(FP8X4),
+                scales=z_scales[:, part],
+                in_=z_woven[h][:].rearrange("p c t -> p (c t)"),
             )
-        for t in range(4):
-            cols = slice(t * P, (t + 1) * P)
-            parts = ((0, 0, HALF), (4, HALF, S)) if t == 0 else ((t, 0, S),)
-            for b, c0, c1 in parts:
+        for t in range(PLANES):
+            places = slice(t * P, (t + 1) * P)
+            for b, c0, c1 in column_parts(t):
                 acc = bank(b, "h_acc%d_%d" % (t, c0))
-                nc.tensor.matmul_mx(
-                    out=acc[:, 0 : c1 - c0], lhsT=w2q[:, cols].bitcast(FP8X4), lhsT_scale=w2s[:, cols],
-                    rhs=zq[:, c0:c1].bitcast(FP8X4), rhs_scale=zs[:, c0:c1], start=True, stop=True,
+                product(
+                    acc[:, 0 : c1 - c0], w2_codes[:, places].bitcast(FP8X4), w2_scales[:, places],
+                    z_codes[:, c0:c1], z_scales[:, c0:c1],
                 )
-                nc.scalar.copy(hw[t][:, c0:c1], acc[:, 0 : c1 - c0])
+                nc.scalar.copy(h_table[t][:, c0:c1], acc[:, 0 : c1 - c0])
                 if c0 == 0:
-                    nc.scalar.copy(ha[:, t, 0:NC], acc[:, 0:NC])
-            nc.sync.dma_start(ha[:, t, NC:S], hw[t][:, NC:S])
+                    nc.scalar.copy(h_plain[:, t, 0:CHUNK], acc[:, 0:CHUNK])
+            nc.sync.dma_start(h_plain[:, t, CHUNK:S], h_table[t][:, CHUNK:S])
 
-        w3w = sb("w3w", [P, 2 * S], U8, tag="zb1")
+        w3_dealt = sb("w3_dealt", [P, 2 * S], U8, tag="z_woven1")
         nc.vector.tensor_copy(
-            w3w[:].rearrange("p (t m e) -> p m t e", t=4, e=2), w3w_raw[:].rearrange("p (m t e) -> p m t e", t=4, e=2)
+            w3_dealt[:].rearrange("p (t m e) -> p m t e", t=PLANES, e=2),
+            w3_words_raw[:].rearrange("p (m t e) -> p m t e", t=PLANES, e=2),
         )
-        w3s = sb("w3s", [P, S], U8, tag="d3")
-        nc.vector.tensor_copy(w3s[:].rearrange("p (t m) -> p m t", t=4), w3s_raw[:].rearrange("p (m t) -> p m t", t=4))
+        w3_scales_dealt = sb("w3_scales_dealt", [P, S], U8, tag="gap3")
+        nc.vector.tensor_copy(
+            w3_scales_dealt[:].rearrange("p (t m) -> p m t", t=PLANES),
+            w3_scales_raw[:].rearrange("p (m t) -> p m t", t=PLANES),
+        )
 
-        oq = sb("oq", [P, S], U32)
-        osc = sb("osc", [P, S], U8)
-        out0v = out_0.rearrange("(p t) c -> p t c", t=4)
-        out1v = out_1[0].rearrange("p c r -> p (c r)").bitcast(I32)
-        accs = []
-        for c0, n in STRETCHES:
-            lists = slice(c0 // 16, (c0 + n) // 16)
-            cols = slice(c0, c0 + n)
-            d1 = sb("d1_%d" % c0, [P, 4, n], F32, tag="d1")
-            d2 = sb("d2_%d" % c0, [P, 4, n], F32, tag="d2")
-            neg = sb("neg%d" % c0, [P, 4, n], F32, tag="pairs%d" % (c0 // NC - 1) if c0 else None)
-            up = sb("up%d" % c0, [P, 4, n], F32, tag="z2b2" if c0 == 384 else None)
-            down = sb("down%d" % c0, [P, 4, n], F32)
-            half = sb("half%d" % c0, [P, 4, n], F32, tag="down%d" % (c0 - NC) if c0 else None)
-            for t in range(4):
-                nc.vector.tensor_tensor(d1[:, t, :], hw[t][:].indirect(n3_t[:, lists]), ha[:, t, cols], ALU.subtract)
-                nc.vector.tensor_tensor(d2[:, t, :], hw[t][:].indirect(n4_t[:, lists]), ha[:, t, cols], ALU.subtract)
+        out_codes = sb("out_codes", [P, S], U32)
+        out_scales = sb("out_scales", [P, S], U8)
+        out_rows = out_0.rearrange("(p t) c -> p t c", t=PLANES)
+        out_words = out_1[0].rearrange("p c r -> p (c r)").bitcast(I32)
+        out_accs = []
+        for c in range(CHUNKS):
+            cols = slice(c * CHUNK, (c + 1) * CHUNK)
+            shape = [P, PLANES, CHUNK]
+            d1 = sb("d1_%d" % c, shape, F32, tag="gap1")
+            d2 = sb("d2_%d" % c, shape, F32, tag="gap2")
+            neg = sb("neg%d" % c, shape, F32, tag="pairs%d" % (c - 1) if c else None)
+            up = sb("up%d" % c, shape, F32, tag="z2_woven%d" % (c - 1) if c == LAST else None)
+            down = sb("down%d" % c, shape, F32)
+            half = sb("half%d" % c, shape, F32, tag="down%d" % (c - 1) if c else None)
+            for t in range(PLANES):
+                here = h_plain[:, t, cols]
+                nc.vector.tensor_tensor(d1[:, t, :], h_table[t][:].indirect(entries_of(n3_t, c)), here, ALU.subtract)
+                nc.vector.tensor_tensor(d2[:, t, :], h_table[t][:].indirect(entries_of(n4_t, c)), here, ALU.subtract)
                 if t % 2:
-                    ts = slice(t - 1, t + 1)
-                    nc.scalar.activation(neg[:, ts, :], d1[:, ts, :], ACT.Relu, scale=-0.5)
-            nc.scalar.activation(half[:], ha[:, :, cols], ACT.Copy, scale=0.5)
-            for g in range(2):
-                ts = slice(2 * g, 2 * g + 2)
-                nc.vector.scalar_tensor_tensor(up[:, ts, :], d1[:, ts, :], 0.0, d2[:, ts, :], ALU.max, ALU.max)
-                nc.vector.scalar_tensor_tensor(down[:, ts, :], d2[:, ts, :], -0.5, neg[:, ts, :], ALU.mult, ALU.max)
-            for s0 in range(0, n, NC):
-                c = (c0 + s0) // NC
-                sub = slice(s0, s0 + NC)
-                pairs = sb("pairs%d" % c, [P, 2, P, 2], BF16)
-                words = pairs[:].rearrange("j u p e -> j (u p e)").bitcast(F32)
-                back = bank(2 + c % 2, "back%d" % c)
-                for u in range(2):
-                    sum_t = bank(u, "sum_t%d_%d" % (c, u))
-                    order = [(term, e) for term in (half, up, down) for e in range(2)]
-                    for k, (term, e) in enumerate(order):
-                        nc.tensor.matmul(
-                            sum_t[:, e * P : (e + 1) * P], term[:, 2 * u + e, sub], ident[:], is_transpose=True,
-                            start=(k == 0), stop=(k == len(order) - 1),
-                        )
-                    nc.scalar.copy(pairs[:, u], sum_t[:, 0 : 2 * P].rearrange("j (e p) -> j p e", e=2))
-                    nc.tensor.transpose(back[:, u * P : (u + 1) * P], words[:, u * P : (u + 1) * P], ident[:])
-                z2b = sb("z2b%d" % c, [P, 4 * NC], BF16)
-                nc.scalar.copy(
-                    z2b[:].bitcast(F32).rearrange("p (j u) -> p j u", u=2),
-                    back[:, 0 : 2 * P].rearrange("p (u j) -> p j u", u=2),
-                )
-                z2q = sb("z2q%d" % c, [P, NC], U32)
-                z2s = sb("z2s%d" % c, [P, NC], U8)
-                nc.vector.quantize_mx(out=z2q[:].bitcast(FP8X4), scales=z2s[:], in_=z2b[:])
-                groups = ((4 + c, 0, 2), (0, 2, 4)) if c == 3 else ((4 + c, 0, 4),)
-                accs.append([])
-                for b, t0, t1 in groups:
-                    acc = bank(b, "o_acc%d_%d" % (c, t0))
-                    for t in range(t0, t1):
-                        nc.tensor.matmul_mx(
-                            out=acc[:, (t - t0) * NC : (t - t0 + 1) * NC],
-                            lhsT=w3w[:, 256 * t : 256 * (t + 1)].bitcast(FP4X4), lhsT_scale=w3s[:, t * P : (t + 1) * P],
-                            rhs=z2q[:].bitcast(FP8X4), rhs_scale=z2s[:], start=True, stop=True,
-                        )
-                    accs[c].append((acc, t0, t1))
-        outs = {}
+                    two = slice(t - 1, t + 1)
+                    nc.scalar.activation(neg[:, two, :], d1[:, two, :], ACT.Relu, scale=-0.5)
+            nc.scalar.activation(half[:], h_plain[:, :, cols], ACT.Copy, scale=0.5)
+            for u in range(2):
+                two = slice(2 * u, 2 * u + 2)
+                nc.vector.scalar_tensor_tensor(up[:, two, :], d1[:, two, :], 0.0, d2[:, two, :], ALU.max, ALU.max)
+                nc.vector.scalar_tensor_tensor(down[:, two, :], d2[:, two, :], -0.5, neg[:, two, :], ALU.mult, ALU.max)
 
-        def add_residual(c, tag):
-            cols = slice(c * NC, (c + 1) * NC)
-            o = sb("o%d" % c, [P, 4, NC], F32, tag=tag)
-            for acc, t0, t1 in accs[c]:
-                sums = acc[:, 0 : (t1 - t0) * NC].rearrange("p (k n) -> p k n", n=NC)
-                nc.vector.tensor_tensor(o[:, t0:t1, :], sums, res_t[:, t0:t1, cols], ALU.add)
-            nc.sync.dma_start(out0v[:, :, cols], o[:])
-            outs[c] = o
-
-        ob = sb("ob", [P, S * 4], BF16, tag="pairs3")
-
-        def round_out(c, copy):
-            interleave(copy, ob[:, 4 * NC * c : 4 * NC * (c + 1)].rearrange("p (c t) -> p c t", t=4), outs[c][:])
-
-        def planes(c0, c1):
-            cols = slice(c0 * NC, c1 * NC)
-            nc.vector.quantize_mx(
-                out=oq[:, cols].bitcast(FP8X4), scales=osc[:, cols], in_=ob[:, 4 * NC * c0 : 4 * NC * c1]
+            pairs = sb("pairs%d" % c, [P, 2, P, 2], BF16)
+            words = pairs[:].rearrange("j u p e -> j (u p e)").bitcast(F32)
+            back = bank(BACK_BANK + c % 2, "back%d" % c)
+            for u in range(2):
+                total = bank(u, "total%d_%d" % (c, u))
+                steps = [(term, e) for term in (half, up, down) for e in range(2)]
+                for k, (term, e) in enumerate(steps):
+                    nc.tensor.matmul(
+                        total[:, e * P : (e + 1) * P], term[:, 2 * u + e, :], ident[:], is_transpose=True,
+                        start=(k == 0), stop=(k == len(steps) - 1),
+                    )
+                nc.scalar.copy(pairs[:, u], total[:, 0 : 2 * P].rearrange("j (e p) -> j p e", e=2))
+                nc.tensor.transpose(back[:, u * P : (u + 1) * P], words[:, u * P : (u + 1) * P], ident[:])
+            z2_woven = sb("z2_woven%d" % c, [P, PLANES * CHUNK], BF16)
+            nc.scalar.copy(
+                z2_woven[:].bitcast(F32).rearrange("p (j u) -> p j u", u=2),
+                back[:, 0 : 2 * P].rearrange("p (u j) -> p j u", u=2),
             )
-            nc.sync.dma_start(out1v[:, cols], oq[:, cols].bitcast(I32))
+            z2_codes = sb("z2_codes%d" % c, [P, CHUNK], U32)
+            z2_scales = sb("z2_scales%d" % c, [P, CHUNK], U8)
+            nc.vector.quantize_mx(out=z2_codes[:].bitcast(FP8X4), scales=z2_scales[:], in_=z2_woven[:])
 
-        add_residual(0, "pairs2")
-        add_residual(1, "d2")
-        add_residual(2, "down384")
-        add_residual(3, None)
-        round_out(3, nc.vector.tensor_copy)
-        planes(3, 4)
-        round_out(0, nc.vector.tensor_copy)
-        round_out(1, nc.scalar.copy)
-        round_out(2, nc.scalar.copy)
-        planes(0, 2)
-        planes(2, 3)
+            if c == LAST:
+                groups = ((OUT_BANK + c, 0, 2), (0, 2, PLANES))
+            else:
+                groups = ((OUT_BANK + c, 0, PLANES),)
+            out_accs.append([])
+            for b, t0, t1 in groups:
+                acc = bank(b, "out_acc%d_%d" % (c, t0))
+                for t in range(t0, t1):
+                    product(
+                        acc[:, (t - t0) * CHUNK : (t - t0 + 1) * CHUNK],
+                        w3_dealt[:, 2 * P * t : 2 * P * (t + 1)].bitcast(FP4X4),
+                        w3_scales_dealt[:, t * P : (t + 1) * P],
+                        z2_codes[:], z2_scales[:],
+                    )
+                out_accs[c].append((acc, t0, t1))
+
+        out_woven = sb("out_woven", [P, S * PLANES], BF16, tag="pairs%d" % LAST)
+        results = []
+        for c, tag in enumerate(("pairs%d" % (LAST - 1), "gap2", "down%d" % LAST, None)):
+            cols = slice(c * CHUNK, (c + 1) * CHUNK)
+            result = sb("result%d" % c, [P, PLANES, CHUNK], F32, tag=tag)
+            for acc, t0, t1 in out_accs[c]:
+                sums = acc[:, 0 : (t1 - t0) * CHUNK].rearrange("p (t n) -> p t n", n=CHUNK)
+                nc.vector.tensor_tensor(result[:, t0:t1, :], sums, res_t[:, t0:t1, cols], ALU.add)
+            nc.sync.dma_start(out_rows[:, :, cols], result[:])
+            results.append(result)
+
+        width = PLANES * CHUNK
+
+        def round_result(c, copy):
+            woven = out_woven[:, width * c : width * (c + 1)].rearrange("p (c t) -> p c t", t=PLANES)
+            interleave(copy, woven, results[c][:])
+
+        def store_planes(first, end):
+            cols = slice(first * CHUNK, end * CHUNK)
+            nc.vector.quantize_mx(
+                out=out_codes[:, cols].bitcast(FP8X4),
+                scales=out_scales[:, cols],
+                in_=out_woven[:, width * first : width * end],
+            )
+            nc.sync.dma_start(out_words[:, cols], out_codes[:, cols].bitcast(I32))
+
+        round_result(LAST, nc.vector.tensor_copy)
+        store_planes(LAST, CHUNKS)
+        round_result(0, nc.vector.tensor_copy)
+        round_result(1, nc.scalar.copy)
+        round_result(2, nc.scalar.copy)
+        store_planes(0, 2)
+        store_planes(2, LAST)
         for q in range(4):
-            eng = nc.scalar if q % 2 else nc.sync
-            eng.dma_start(out_2[0, 4 * q : 4 * q + 4, :].bitcast(I32), osc[32 * q : 32 * q + 4, :].bitcast(I32))
+            queue = nc.scalar if q % 2 else nc.sync
+            queue.dma_start(
+                out_2[0, 4 * q : 4 * q + 4, :].bitcast(I32), out_scales[32 * q : 32 * q + 4, :].bitcast(I32)
+            )

from contextlib import ExitStack

import concourse.mybir as mybir
from concourse.masks import make_identity

F32 = mybir.dt.float32
BF16 = mybir.dt.bfloat16
I32 = mybir.dt.int32
U32 = mybir.dt.uint32
U16 = mybir.dt.uint16
U8 = mybir.dt.uint8
FP8X4 = mybir.dt.float8_e4m3fn_x4
FP4X4 = mybir.dt.float4_e2m1fn_x4
ALU = mybir.AluOpType
ACT = mybir.ActivationFunctionType

P = 128
PLANES = 4
TOKENS = 2048
S = 512
PAIRS = 256
HALF = S // 2
CHUNK = 128
CHUNKS = S // CHUNK
LAST = CHUNKS - 1
PER_COLUMN = 16
SCALE_ROWS = 16
W1_VECTOR_SHARE = 44
Z_SCALAR_SHARE = 192
SPARE_BANK = 4
OUT_BANK = 4
BACK_BANK = 2

FLOPS = 805306368


def tile_picked_deepfillrange_none_po_kernel(
    tc, x_words, x_scales, w1, w2, w3_words, w3_scales, res, offs, n1, n2, n3, n4, out_0, out_1, out_2
):
    nc = tc.nc
    with ExitStack() as ctx:
        keep = ctx.enter_context(tc.tile_pool(name="keep", bufs=1))
        psum = ctx.enter_context(tc.psum_pool(name="psum", bufs=1))

        def sb(name, shape, dtype, tag=None):
            return keep.tile(shape, dtype, name=name, tag=tag or name, align_bytes=64)

        def bank(i, name):
            return psum.tile([P, S], F32, name=name, tag="bank%d" % i)

        def load_list(name, src, entries):
            lists = keep.tile([P, entries // PER_COLUMN], U16, name=name)
            nc.sync.dma_start(lists[:], src)
            return lists

        def entries_of(lists, c):
            return lists[:, c * CHUNK // PER_COLUMN : (c + 1) * CHUNK // PER_COLUMN]

        def interleave(copy, dst, src):
            copy(dst.rearrange("p (c i) t -> p c t i", i=4), src.rearrange("p t (c i) -> p c t i", i=4))

        def round_and_deal(copy, dst, src):
            copy(dst.rearrange("p t m j -> p m t j"), src.rearrange("p j (m t) -> p m t j", t=PLANES))

        def product(acc, weights, weight_scales, codes, scales):
            nc.tensor.matmul_mx(
                out=acc, lhsT=weights, lhsT_scale=weight_scales, rhs=codes.bitcast(FP8X4), rhs_scale=scales,
                start=True, stop=True,
            )

        def column_parts(t):
            return ((0, 0, HALF), (SPARE_BANK, HALF, S)) if t == 0 else ((t, 0, S),)

        x_scale_table = sb("x_scale_table", [P, TOKENS], U8)
        for p0, p1 in ((0, SCALE_ROWS), (32, 64), (64, P)):
            nc.vector.memset(x_scale_table[p0:p1, :].bitcast(I32), 0)
        picked_scales = sb("picked_scales", [P, S], U8)
        nc.gpsimd.memset(picked_scales[:].bitcast(I32), 0)
        ident = sb("ident", [P, P], F32)
        make_identity(nc, ident[:])
        w3_scales_raw = sb("w3_scales_raw", [P, S], U8)
        nc.gpsimd.memset(w3_scales_raw[:].bitcast(I32), 0)

        offs_t = load_list("offs_t", offs, S)
        nc.sync.dma_start(x_scale_table[SCALE_ROWS : 2 * SCALE_ROWS, :].bitcast(I32), x_scales[0].bitcast(I32))
        x_word_table = sb("x_word_table", [P, TOKENS], U32)
        nc.sync.dma_start(x_word_table[:].bitcast(I32), x_words[0].rearrange("p c r -> p (c r)").bitcast(I32))
        w1_rows = w1.rearrange("(p j) c -> p j c", j=PLANES)
        w1_raw = sb("w1_raw", [P, 2, PLANES, HALF], F32)
        for h in range(2):
            nc.sync.dma_start(w1_raw[:, h], w1_rows[:, :, h * HALF : (h + 1) * HALF])
        n1_t = load_list("n1_t", n1, PAIRS)
        n2_t = load_list("n2_t", n2, PAIRS)
        n3_t = load_list("n3_t", n3, S)
        n4_t = load_list("n4_t", n4, S)

        picked_rows = sb("picked_rows", [P, S], U8)
        nc.vector.tensor_copy(picked_rows[:], x_scale_table[:].indirect(offs_t[:]))
        for q in range(4):
            nc.scalar.dma_start(
                picked_scales[32 * q : 32 * q + 4, :].bitcast(I32),
                picked_rows[SCALE_ROWS + 4 * q : SCALE_ROWS + 4 * q + 4, :].bitcast(I32),
            )
        picked_words = sb("picked_words", [P, S], U32)
        nc.vector.tensor_copy(picked_words[:], x_word_table[:].indirect(offs_t[:]))

        w1_bf = sb("w1_bf", [P, PLANES, P, PLANES], BF16)
        per_half = HALF // PLANES
        for h, m0, m1, copy in (
            (0, 0, per_half, nc.vector.tensor_copy),
            (1, 0, W1_VECTOR_SHARE, nc.vector.tensor_copy),
            (1, W1_VECTOR_SHARE, per_half, nc.scalar.copy),
        ):
            round_and_deal(
                copy,
                w1_bf[:, :, per_half * h + m0 : per_half * h + m1, :],
                w1_raw[:, h, :, PLANES * m0 : PLANES * m1],
            )
        w1_codes = sb("w1_codes", [P, S], U32)
        w1_scales = sb("w1_scales", [P, S], U8)
        w1_flat = w1_bf[:].rearrange("p t m j -> p (t m j)")
        for t0, t1 in ((0, 1), (1, 2), (2, PLANES)):
            nc.vector.quantize_mx(
                out=w1_codes[:, P * t0 : P * t1].bitcast(FP8X4),
                scales=w1_scales[:, P * t0 : P * t1],
                in_=w1_flat[:, S * t0 : S * t1],
            )

        w2_raw = sb("w2_raw", [P, PLANES, S], F32, tag="w1_raw")
        nc.sync.dma_start(w2_raw[:], w2.rearrange("(p j) c -> p j c", j=PLANES))
        w3_words_raw = sb("w3_words_raw", [P, 2 * S], U8, tag="w1_bf")
        nc.sync.dma_start(w3_words_raw[:].bitcast(I32), w3_words[0].bitcast(I32))
        for q in range(4):
            nc.sync.dma_start(
                w3_scales_raw[32 * q : 32 * q + 4, :].bitcast(I32), w3_scales[0, 4 * q : 4 * q + 4, :].bitcast(I32)
            )
        w2_bf = sb("w2_bf", [P, PLANES, P, PLANES], BF16)
        per_piece = P // 4
        for k in range(4):
            round_and_deal(
                nc.scalar.copy,
                w2_bf[:, :, per_piece * k : per_piece * (k + 1), :],
                w2_raw[:, :, PLANES * per_piece * k : PLANES * per_piece * (k + 1)],
            )
        res_t = sb("res_t", [P, PLANES, S], F32, tag="w1_raw")
        nc.sync.dma_start(res_t[:], res.rearrange("(p t) c -> p t c", t=PLANES))

        z_planes = []
        for t in range(PLANES):
            places = slice(t * P, (t + 1) * P)
            y = sb("y%d" % t, [P, S], F32)
            for b, c0, c1 in column_parts(t):
                acc = bank(b, "y_acc%d_%d" % (t, c0))
                product(
                    acc[:, 0 : c1 - c0], w1_codes[:, places].bitcast(FP8X4), w1_scales[:, places],
                    picked_words[:, c0:c1], picked_scales[:, c0:c1],
                )
                copy = nc.vector.tensor_copy if b == SPARE_BANK else nc.scalar.copy
                copy(y[:, c0:c1], acc[:, 0 : c1 - c0])
            pa = sb("pa%d" % t, [P, PAIRS], F32)
            gap = sb("gap%d" % t, [P, PAIRS], F32)
            rise = sb("rise%d" % t, [P, PAIRS], F32)
            for k in range(2):
                nc.vector.tensor_copy(pa[:, k * CHUNK : (k + 1) * CHUNK], y[:].indirect(entries_of(n1_t, k)))
            for k in range(2):
                part = slice(k * CHUNK, (k + 1) * CHUNK)
                nc.vector.tensor_tensor(gap[:, part], y[:].indirect(entries_of(n2_t, k)), pa[:, part], ALU.subtract)
            nc.scalar.activation(rise[:], gap[:], ACT.Relu)
            nc.vector.tensor_tensor(y[:].indirect(n1_t[:]), pa[:], rise[:], ALU.add)
            z_planes.append(y)

        z_bf = sb("z_bf", [P, PLANES, S], BF16, tag="gap3")
        for t in range(PLANES - 1):
            nc.scalar.copy(z_bf[:, t, :], z_planes[t][:])
        for h in range(2):
            part = slice(h * HALF, (h + 1) * HALF)
            nc.scalar.copy(z_bf[:, PLANES - 1, part], z_planes[PLANES - 1][:, part])

        w2_codes = sb("w2_codes", [P, S], U32, tag="pa3")
        w2_scales = sb("w2_scales", [P, S], U8)
        nc.vector.quantize_mx(
            out=w2_codes[:].bitcast(FP8X4), scales=w2_scales[:], in_=w2_bf[:].rearrange("p t m j -> p (t m j)")
        )

        z_woven = [sb("z_woven%d" % h, [P, HALF, PLANES], BF16) for h in range(2)]
        interleave(nc.vector.tensor_copy, z_woven[0][:], z_bf[:, :, 0:HALF])
        interleave(nc.scalar.copy, z_woven[1][:, 0:Z_SCALAR_SHARE, :], z_bf[:, :, HALF : HALF + Z_SCALAR_SHARE])
        interleave(nc.vector.tensor_copy, z_woven[1][:, Z_SCALAR_SHARE:HALF, :], z_bf[:, :, HALF + Z_SCALAR_SHARE : S])
        h_table = [sb("h_table%d" % t, [P, S], F32) for t in range(PLANES)]
        h_plain = sb("h_plain", [P, PLANES, S], F32)
        z_codes = sb("z_codes", [P, S], U32)
        z_scales = sb("z_scales", [P, S], U8)
        for h in range(2):
            part = slice(h * HALF, (h + 1) * HALF)
            nc.vector.quantize_mx(
                out=z_codes[:, part].bitcast(FP8X4),
                scales=z_scales[:, part],
                in_=z_woven[h][:].rearrange("p c t -> p (c t)"),
            )
        for t in range(PLANES):
            places = slice(t * P, (t + 1) * P)
            for b, c0, c1 in column_parts(t):
                acc = bank(b, "h_acc%d_%d" % (t, c0))
                product(
                    acc[:, 0 : c1 - c0], w2_codes[:, places].bitcast(FP8X4), w2_scales[:, places],
                    z_codes[:, c0:c1], z_scales[:, c0:c1],
                )
                nc.scalar.copy(h_table[t][:, c0:c1], acc[:, 0 : c1 - c0])
                if c0 == 0:
                    nc.scalar.copy(h_plain[:, t, 0:CHUNK], acc[:, 0:CHUNK])
            nc.sync.dma_start(h_plain[:, t, CHUNK:S], h_table[t][:, CHUNK:S])

        w3_dealt = sb("w3_dealt", [P, 2 * S], U8, tag="z_woven1")
        nc.vector.tensor_copy(
            w3_dealt[:].rearrange("p (t m e) -> p m t e", t=PLANES, e=2),
            w3_words_raw[:].rearrange("p (m t e) -> p m t e", t=PLANES, e=2),
        )
        w3_scales_dealt = sb("w3_scales_dealt", [P, S], U8, tag="gap3")
        nc.vector.tensor_copy(
            w3_scales_dealt[:].rearrange("p (t m) -> p m t", t=PLANES),
            w3_scales_raw[:].rearrange("p (m t) -> p m t", t=PLANES),
        )

        out_codes = sb("out_codes", [P, S], U32)
        out_scales = sb("out_scales", [P, S], U8)
        out_rows = out_0.rearrange("(p t) c -> p t c", t=PLANES)
        out_words = out_1[0].rearrange("p c r -> p (c r)").bitcast(I32)
        out_accs = []
        for c in range(CHUNKS):
            cols = slice(c * CHUNK, (c + 1) * CHUNK)
            shape = [P, PLANES, CHUNK]
            d1 = sb("d1_%d" % c, shape, F32, tag="gap1")
            d2 = sb("d2_%d" % c, shape, F32, tag="gap2")
            neg = sb("neg%d" % c, shape, F32, tag="pairs%d" % (c - 1) if c else None)
            up = sb("up%d" % c, shape, F32, tag="z2_woven%d" % (c - 1) if c == LAST else None)
            down = sb("down%d" % c, shape, F32)
            half = sb("half%d" % c, shape, F32, tag="down%d" % (c - 1) if c else None)
            for t in range(PLANES):
                here = h_plain[:, t, cols]
                nc.vector.tensor_tensor(d1[:, t, :], h_table[t][:].indirect(entries_of(n3_t, c)), here, ALU.subtract)
                nc.vector.tensor_tensor(d2[:, t, :], h_table[t][:].indirect(entries_of(n4_t, c)), here, ALU.subtract)
                if t % 2:
                    two = slice(t - 1, t + 1)
                    nc.scalar.activation(neg[:, two, :], d1[:, two, :], ACT.Relu, scale=-0.5)
            nc.scalar.activation(half[:], h_plain[:, :, cols], ACT.Copy, scale=0.5)
            for u in range(2):
                two = slice(2 * u, 2 * u + 2)
                nc.vector.scalar_tensor_tensor(up[:, two, :], d1[:, two, :], 0.0, d2[:, two, :], ALU.max, ALU.max)
                nc.vector.scalar_tensor_tensor(down[:, two, :], d2[:, two, :], -0.5, neg[:, two, :], ALU.mult, ALU.max)

            pairs = sb("pairs%d" % c, [P, 2, P, 2], BF16)
            words = pairs[:].rearrange("j u p e -> j (u p e)").bitcast(F32)
            back = bank(BACK_BANK + c % 2, "back%d" % c)
            for u in range(2):
                total = bank(u, "total%d_%d" % (c, u))
                steps = [(term, e) for term in (half, up, down) for e in range(2)]
                for k, (term, e) in enumerate(steps):
                    nc.tensor.matmul(
                        total[:, e * P : (e + 1) * P], term[:, 2 * u + e, :], ident[:], is_transpose=True,
                        start=(k == 0), stop=(k == len(steps) - 1),
                    )
                nc.scalar.copy(pairs[:, u], total[:, 0 : 2 * P].rearrange("j (e p) -> j p e", e=2))
                nc.tensor.transpose(back[:, u * P : (u + 1) * P], words[:, u * P : (u + 1) * P], ident[:])
            z2_woven = sb("z2_woven%d" % c, [P, PLANES * CHUNK], BF16)
            nc.scalar.copy(
                z2_woven[:].bitcast(F32).rearrange("p (j u) -> p j u", u=2),
                back[:, 0 : 2 * P].rearrange("p (u j) -> p j u", u=2),
            )
            z2_codes = sb("z2_codes%d" % c, [P, CHUNK], U32)
            z2_scales = sb("z2_scales%d" % c, [P, CHUNK], U8)
            nc.vector.quantize_mx(out=z2_codes[:].bitcast(FP8X4), scales=z2_scales[:], in_=z2_woven[:])

            if c == LAST:
                groups = ((OUT_BANK + c, 0, 2), (0, 2, PLANES))
            else:
                groups = ((OUT_BANK + c, 0, PLANES),)
            out_accs.append([])
            for b, t0, t1 in groups:
                acc = bank(b, "out_acc%d_%d" % (c, t0))
                for t in range(t0, t1):
                    product(
                        acc[:, (t - t0) * CHUNK : (t - t0 + 1) * CHUNK],
                        w3_dealt[:, 2 * P * t : 2 * P * (t + 1)].bitcast(FP4X4),
                        w3_scales_dealt[:, t * P : (t + 1) * P],
                        z2_codes[:], z2_scales[:],
                    )
                out_accs[c].append((acc, t0, t1))

        out_woven = sb("out_woven", [P, S * PLANES], BF16, tag="pairs%d" % LAST)
        results = []
        for c, tag in enumerate(("pairs%d" % (LAST - 1), "gap2", "down%d" % LAST, None)):
            cols = slice(c * CHUNK, (c + 1) * CHUNK)
            result = sb("result%d" % c, [P, PLANES, CHUNK], F32, tag=tag)
            for acc, t0, t1 in out_accs[c]:
                sums = acc[:, 0 : (t1 - t0) * CHUNK].rearrange("p (t n) -> p t n", n=CHUNK)
                nc.vector.tensor_tensor(result[:, t0:t1, :], sums, res_t[:, t0:t1, cols], ALU.add)
            nc.sync.dma_start(out_rows[:, :, cols], result[:])
            results.append(result)

        width = PLANES * CHUNK

        def round_result(c, copy):
            woven = out_woven[:, width * c : width * (c + 1)].rearrange("p (c t) -> p c t", t=PLANES)
            interleave(copy, woven, results[c][:])

        def store_planes(first, end):
            cols = slice(first * CHUNK, end * CHUNK)
            nc.vector.quantize_mx(
                out=out_codes[:, cols].bitcast(FP8X4),
                scales=out_scales[:, cols],
                in_=out_woven[:, width * first : width * end],
            )
            nc.sync.dma_start(out_words[:, cols], out_codes[:, cols].bitcast(I32))

        round_result(LAST, nc.vector.tensor_copy)
        store_planes(LAST, CHUNKS)
        round_result(0, nc.vector.tensor_copy)
        round_result(1, nc.scalar.copy)
        round_result(2, nc.scalar.copy)
        store_planes(0, 2)
        store_planes(2, LAST)
        for q in range(4):
            queue = nc.scalar if q % 2 else nc.sync
            queue.dma_start(
                out_2[0, 4 * q : 4 * q + 4, :].bitcast(I32), out_scales[32 * q : 32 * q + 4, :].bitcast(I32)
            )
